import numpy as np
import ml_dtypes


def mxq(x, axis, fmt="e4m3"):
    dtype, down = {"e4m3": (ml_dtypes.float8_e4m3fn, 7), "e5m2": (ml_dtypes.float8_e5m2, 14)}[fmt]
    v = np.moveaxis(np.asarray(x, np.float32).astype(ml_dtypes.bfloat16).astype(np.float64), axis, -1)
    blocks = v.reshape(v.shape[:-1] + (-1, 32))
    amax = np.abs(blocks).max(-1, keepdims=True)
    byte = np.maximum(np.where(amax > 0, np.frexp(amax)[1] - 1 + 127, 0) - down, 1)
    scale = np.exp2(byte - 127.0)
    codes = (blocks / scale).astype(np.float32).astype(dtype).astype(np.float64)
    return np.moveaxis((codes * scale).reshape(v.shape), -1, axis)


WIDE = False


def mx_kscale(k):
    if not WIDE:
        return np.ones(k)
    levels = np.array([10, -10, 5, -5, 0])
    if k % 512:
        return np.exp2(np.random.permutation(np.resize(levels, k // 32))).repeat(32)
    a = np.empty((k // 512, 16))
    for p in range(k // 512):
        a[p, :8] = np.random.permutation(np.resize(levels, 8))
        for g in range(8):
            far = levels[np.abs(levels - a[p, g]) >= 10]
            a[p, g + 8] = far[np.random.randint(len(far))]
    return np.exp2(a.ravel()).repeat(32)


def f64(x):
    return np.asarray(x).astype(np.float64)


def striped(idx):
    return np.tile(idx.reshape(-1, 16).T, (8, 1)).astype(np.uint16)


def unstriped(offs):
    return offs[:16].T.reshape(-1).astype(np.int64)


E2M1 = np.array([0.0, 0.5, 1.0, 1.5, 2.0, 3.0, 4.0, 6.0, -0.0, -0.5, -1.0, -1.5, -2.0, -3.0, -4.0, -6.0])


def pack_weight(w, fmt):
    k, n = w.shape
    w = f64(np.asarray(w, np.float32).astype(ml_dtypes.bfloat16)).reshape(k // 32, 32, n)
    amax = np.abs(w).max(1)
    if fmt == "e4m3":
        byte = np.frexp(amax)[1] - 1 + 127 - 7
    else:
        mant, ex = np.frexp(amax / 6.0)
        byte = np.where(mant > 0.5, ex, ex - 1) + 127
    byte = np.clip(np.where(amax > 0, byte, 1), 1, 254)
    scaled = (w * np.exp2(127.0 - byte)[:, None, :]).reshape(k, n).astype(np.float32)
    by_word = np.ascontiguousarray(scaled.reshape(k // 512, 128, 4, n).transpose(0, 1, 3, 2))
    if fmt == "e4m3":
        words = by_word.astype(ml_dtypes.float8_e4m3fn).view(np.uint8)
    else:
        c = by_word.astype(ml_dtypes.float4_e2m1fn).view(np.uint8) & 0xF
        words = (c[..., 0::2] | (c[..., 1::2] << 4)).reshape(k // 512, 128, 2 * n)
    return np.ascontiguousarray(words), np.ascontiguousarray(byte.astype(np.uint8).reshape(k // 512, 16, n))


def unpack_weight(words, scales, fmt):
    g, _, n = scales.shape
    words = np.ascontiguousarray(words).reshape(g, 128, n, -1)
    if fmt == "e4m3":
        vals = words.view(ml_dtypes.float8_e4m3fn).astype(np.float64)
    else:
        nib = np.empty((g, 128, n, 4), np.uint8)
        nib[..., 0::2] = words & 0xF
        nib[..., 1::2] = words >> 4
        vals = E2M1[nib]
    vals = vals * np.repeat(np.exp2(scales.astype(np.float64) - 127.0), 8, axis=1)[..., None]
    return vals.transpose(0, 1, 3, 2).reshape(g * 512, n)


def gelu(v):
    return 0.5 * v * (1.0 + np.tanh(np.sqrt(2.0 / np.pi) * (v + 0.044715 * v**3)))


K, T, S, H, T2, S2 = 1024, 2048, 512, 1024, 4096, 1536

def setup_inputs():
    n = np.random.standard_normal
    s = mx_kscale(K)[:, None]
    u = mx_kscale(H)[:, None]
    tab_words, tab_scales = pack_weight(n((K, T)) * s, "e4m3")
    tab2_words, tab2_scales = pack_weight(np.tanh(n((H, T2))) / np.sqrt(H) / u, "e4m3")
    w4_words, w4_scales = pack_weight(n((K, H)) / np.sqrt(K) / s * u.T, "e2m1")
    return {
        "tab_words": tab_words, "tab_scales": tab_scales,
        "offs": striped(np.random.permutation(T)[:S]),
        "tab2_words": tab2_words, "tab2_scales": tab2_scales,
        "offs2": striped(np.random.permutation(T2)[:S2]),
        "w1": (n((K, H)) / np.sqrt(K) / s).astype(np.float32),
        "gain": np.exp(0.3 * n(H)).astype(np.float32),
        "w4_words": w4_words, "w4_scales": w4_scales,
    }

def reference(tab_words, tab_scales, offs, tab2_words, tab2_scales, offs2, w1, gain, w4_words, w4_scales):
    v = unpack_weight(tab_words, tab_scales, "e4m3")[:, unstriped(offs)]
    v2 = unpack_weight(tab2_words, tab2_scales, "e4m3")[:, unstriped(offs2)]
    w4 = unpack_weight(w4_words, w4_scales, "e2m1")
    p = mxq(f64(w1), 0, "e4m3").T @ v
    c = w4.T @ v
    h = c * np.tanh(p * f64(gain)[:, None])
    y = v2.T @ mxq(h, 0, "e4m3")
    return np.abs(y)

@@ -1,0 +1,196 @@
+from contextlib import ExitStack
+
+import concourse.mybir as mybir
+
+K, T, S, H, T2, S2 = 1024, 2048, 512, 1024, 4096, 1536
+FLOPS = 2 * (2 * K * H * S + H * S2 * S)
+
+F32 = mybir.dt.float32
+BF16 = mybir.dt.bfloat16
+I32 = mybir.dt.int32
+U32 = mybir.dt.uint32
+U16 = mybir.dt.uint16
+U8 = mybir.dt.uint8
+FP8X4 = mybir.dt.float8_e4m3fn_x4
+FP4X4 = mybir.dt.float4_e2m1fn_x4
+ACT = mybir.ActivationFunctionType
+MULT = mybir.AluOpType.mult
+
+P = 128
+HALF = 256
+GROUP = 512
+
+
+def tile_list_duplicate_collision_score_kernel(
+    tc, tab_words, tab_scales, offs, tab2_words, tab2_scales, offs2, w1, gain, w4_words, w4_scales, out
+):
+    nc = tc.nc
+    with ExitStack() as ctx:
+        lists = ctx.enter_context(tc.tile_pool(name="lists", bufs=1))
+        keep = ctx.enter_context(tc.tile_pool(name="keep", bufs=1))
+        ring = ctx.enter_context(tc.tile_pool(name="ring", bufs=3))
+        stage = ctx.enter_context(tc.tile_pool(name="stage", bufs=6))
+        psum = ctx.enter_context(tc.psum_pool(name="psum", bufs=4))
+
+        idx = lists.tile([P, S // 16], U16, name="idx")
+        idx2 = lists.tile([P, S2 // 16], U16, name="idx2")
+
+        s2win = keep.tile([P, T2 // 4], I32, name="s2win", align_bytes=64)
+        w4s_raw = keep.tile([P, 2, H // 4], I32, name="w4s_raw", align_bytes=64)
+        s1win = keep.tile([P, 2, T // 4], I32, name="s1win", align_bytes=64)
+        w4_raw = keep.tile([P, 2, H // 2], I32, name="w4_raw", align_bytes=64)
+        gains = keep.tile([P, 2, 4], F32, name="gains")
+        zero_in = keep.tile([P, 1], F32, name="zero_in")
+        zero = keep.tile([P, 1], F32, name="zero")
+        w1_raw = {(g, a): keep.tile([P, 4, GROUP], F32, name="w1_raw%d%d" % (g, a)) for g in range(2) for a in range(2)}
+        win1 = [keep.tile([P, T], I32, name="win1_%d" % g, align_bytes=64) for g in range(2)]
+        win2 = [keep.tile([P, T2], I32, name="win2_%d" % a, align_bytes=64) for a in range(2)]
+
+        w4c = keep.tile([P, 4 * 4 * 2 * P], U8, name="w4c", align_bytes=64)
+        w4s = keep.tile([P, 4 * 4 * P], U8, name="w4s", align_bytes=64)
+        w1c = keep.tile([P, 4 * 4 * P], U32, name="w1c", align_bytes=64)
+        w1s = keep.tile([P, 4 * 4 * P], U8, name="w1s", align_bytes=64)
+        vc = keep.tile([P, 2, S], U32, name="vc", align_bytes=64)
+        vs = keep.tile([P, 2, S], U8, name="vs", align_bytes=64)
+        v2c = keep.tile([P, 2, S2], U32, name="v2c", align_bytes=64)
+        v2s = keep.tile([P, S2], U8, name="v2s", align_bytes=64)
+        hc = keep.tile([P, 2, S], U32, name="hc", align_bytes=64)
+        hs = keep.tile([P, 2, S], U8, name="hs", align_bytes=64)
+
+        nc.vector.memset(s2win[:], 0)
+        nc.vector.memset(w4s_raw[:], 0)
+        nc.vector.memset(s1win[:], 0)
+        nc.gpsimd.memset(zero_in[:], 0.0)
+        nc.scalar.activation(zero[:], zero_in[:], ACT.Tanh)
+
+        def load_w1(g, a):
+            rows = w1[g * GROUP : (g + 1) * GROUP, a * GROUP : (a + 1) * GROUP]
+            nc.sync.dma_start(out=w1_raw[g, a][:], in_=rows.rearrange("(p j) c -> p j c", j=4))
+
+        def load_words(dst, src):
+            nc.sync.dma_start(out=dst[:], in_=src.rearrange("p t i -> p (t i)").bitcast(I32))
+
+        def load_planes(dst, src):
+            for r in range(4):
+                nc.sync.dma_start(out=dst[r:P:32, :, :], in_=src[:, r:16:4, :].rearrange("g q n -> q g n").bitcast(I32))
+
+        nc.sync.dma_start(idx2[:], offs2)
+        nc.sync.dma_start(out=w4_raw[:], in_=w4_words.rearrange("g p n -> p g n").bitcast(I32))
+        nc.sync.dma_start(idx[:], offs)
+        nc.sync.dma_start(out=gains[:], in_=gain.rearrange("(a p t) -> p a t", a=2, t=4))
+        for a in range(2):
+            for r in range(4):
+                nc.sync.dma_start(out=s2win[4 + 4 * a + r : P : 32, :], in_=tab2_scales[a, r:16:4, :].bitcast(I32))
+        load_w1(0, 0)
+        load_planes(w4s_raw, w4_scales)
+        load_w1(1, 0)
+        load_planes(s1win, tab_scales)
+        load_words(win1[0], tab_words[0])
+        load_w1(0, 1)
+        load_words(win1[1], tab_words[1])
+        load_w1(1, 1)
+        load_words(win2[0], tab2_words[0])
+        load_words(win2[1], tab2_words[1])
+
+        def gather(dst, window, offsets, lo, hi):
+            nc.vector.tensor_copy(dst[:, lo:hi], window.indirect(offsets[:, lo // 16 : hi // 16]))
+
+        nc.vector.tensor_copy(
+            out=w4c[:].bitcast(U16).rearrange("p (b t m) -> p b t m", b=4, t=4),
+            in_=w4_raw[:].rearrange("p g w -> p (g w)").bitcast(U16).rearrange("p (b m t) -> p b t m", b=4, t=4),
+        )
+        for q in range(3):
+            gather(v2s, s2win[:].bitcast(U8), idx2, q * GROUP, (q + 1) * GROUP)
+        nc.vector.tensor_copy(
+            out=w4s[:].rearrange("p (b t m) -> p b t m", b=4, t=4),
+            in_=w4s_raw[:].rearrange("p g w -> p (g w)").bitcast(U8).rearrange("p (b m t) -> p b t m", b=4, t=4),
+        )
+
+        def quantise_w1(g, a):
+            for u in range(2):
+                grouped = ring.tile([P, 2 * GROUP], BF16, name="grouped", align_bytes=64)
+                nc.scalar.copy(
+                    out=grouped[:].rearrange("p (e m j) -> p m j e", e=2, j=4),
+                    in_=w1_raw[g, a][:].rearrange("p j (m t) -> p m j t", t=4)[:, :, :, 2 * u : 2 * u + 2],
+                )
+                c0 = (2 * g + a) * GROUP + u * HALF
+                nc.vector.quantize_mx(out=w1c[:, c0 : c0 + HALF].bitcast(FP8X4), scales=w1s[:, c0 : c0 + HALF], in_=grouped[:])
+
+        quantise_w1(0, 0)
+        for g in range(2):
+            gather(vs[:, g, :], s1win[:, g, :].bitcast(U8), idx, 0, S)
+        quantise_w1(1, 0)
+        gather(vc[:, 0, :], win1[0][:].bitcast(U32), idx, 0, S)
+        quantise_w1(0, 1)
+        for hf in range(2):
+            gather(vc[:, 1, :], win1[1][:].bitcast(U32), idx, hf * HALF, (hf + 1) * HALF)
+
+        def soft_codes(a, hf):
+            tok = slice(hf * HALF, (hf + 1) * HALF)
+            th = ring.tile([P, 4, HALF], F32, name="th")
+            for u in range(2):
+                pb = psum.tile([P, 2, HALF], F32, name="bank_a")
+                for e in range(2):
+                    for g in range(2):
+                        c0 = (2 * g + a) * GROUP + (2 * u + e) * P
+                        nc.tensor.matmul_mx(
+                            out=pb[:, e, :],
+                            lhsT=w1c[:, c0 : c0 + P].bitcast(FP8X4),
+                            lhsT_scale=w1s[:, c0 : c0 + P],
+                            rhs=vc[:, g, tok].bitcast(FP8X4),
+                            rhs_scale=vs[:, g, tok],
+                            start=(g == 0),
+                            stop=(g == 1),
+                        )
+                for e in range(2):
+                    t = 2 * u + e
+                    nc.scalar.activation(th[:, t, :], pb[:, e, :], ACT.Tanh, bias=zero[:], scale=gains[:, a, t : t + 1])
+            hb = ring.tile([P, 4 * HALF], BF16, name="hb", align_bytes=64)
+            for b in range(2):
+                blk = slice(hf * HALF + b * P, hf * HALF + (b + 1) * P)
+                cb = psum.tile([P, 4, P], F32, name="bank_b")
+                for t in range(4):
+                    for g in range(2):
+                        c0 = (2 * g + a) * GROUP + t * P
+                        nc.tensor.matmul_mx(
+                            out=cb[:, t, :],
+                            lhsT=w4c[:, 2 * c0 : 2 * (c0 + P)].bitcast(FP4X4),
+                            lhsT_scale=w4s[:, c0 : c0 + P],
+                            rhs=vc[:, g, blk].bitcast(FP8X4),
+                            rhs_scale=vs[:, g, blk],
+                            start=(g == 0),
+                            stop=(g == 1),
+                        )
+                nc.vector.tensor_tensor(
+                    out=hb[:, b * GROUP : (b + 1) * GROUP].rearrange("p (c i t) -> p c t i", i=4, t=4),
+                    in0=cb[:].rearrange("p t (c i) -> p c t i", i=4),
+                    in1=th[:, :, b * P : (b + 1) * P].rearrange("p t (c i) -> p c t i", i=4),
+                    op=MULT,
+                )
+            nc.vector.quantize_mx(out=hc[:, a, tok].bitcast(FP8X4), scales=hs[:, a, tok], in_=hb[:])
+
+        soft_codes(0, 0)
+        soft_codes(0, 1)
+        quantise_w1(1, 1)
+        soft_codes(1, 0)
+        soft_codes(1, 1)
+
+        for q in range(3):
+            for a in range(2):
+                gather(v2c[:, a, :], win2[a][:].bitcast(U32), idx2, q * GROUP, (q + 1) * GROUP)
+            for n in range(4):
+                rows = slice(q * GROUP + n * P, q * GROUP + (n + 1) * P)
+                yb = psum.tile([P, S], F32, name="bank_a" if n % 2 == 0 else "bank_b")
+                for a in range(2):
+                    nc.tensor.matmul_mx(
+                        out=yb[:],
+                        lhsT=v2c[:, a, rows].bitcast(FP8X4),
+                        lhsT_scale=v2s[4 + 4 * a : P, rows],
+                        rhs=hc[:, a, :].bitcast(FP8X4),
+                        rhs_scale=hs[:, a, :],
+                        start=(a == 0),
+                        stop=(a == 1),
+                    )
+                score = stage.tile([P, S], F32, name="score")
+                nc.scalar.activation(score[:], yb[:], ACT.Abs)
+                nc.sync.dma_start(out=out[rows, :], in_=score[:])

@@ -57,8 +57,8 @@ def tile_list_duplicate_collision_score_kernel(
         hc = keep.tile([P, 2, S], U32, name="hc", align_bytes=64)
         hs = keep.tile([P, 2, S], U8, name="hs", align_bytes=64)
 
-        nc.vector.memset(s2win[:], 0)
         nc.vector.memset(w4s_raw[:], 0)
+        nc.vector.memset(s2win[:], 0)
         nc.vector.memset(s1win[:], 0)
         nc.gpsimd.memset(zero_in[:], 0.0)
         nc.scalar.activation(zero[:], zero_in[:], ACT.Tanh)
@@ -67,67 +67,68 @@ def tile_list_duplicate_collision_score_kernel(
             rows = w1[g * GROUP : (g + 1) * GROUP, a * GROUP : (a + 1) * GROUP]
             nc.sync.dma_start(out=w1_raw[g, a][:], in_=rows.rearrange("(p j) c -> p j c", j=4))
 
-        def load_words(dst, src):
-            nc.sync.dma_start(out=dst[:], in_=src.rearrange("p t i -> p (t i)").bitcast(I32))
+        def load_words(dst, src, lo, hi):
+            nc.sync.dma_start(out=dst[:, lo:hi], in_=src.rearrange("p t i -> p (t i)").bitcast(I32)[:, lo:hi])
 
-        def load_planes(dst, src):
+        def load_planes(queue, dst, src):
             for r in range(4):
-                nc.sync.dma_start(out=dst[r:P:32, :, :], in_=src[:, r:16:4, :].rearrange("g q n -> q g n").bitcast(I32))
+                queue.dma_start(out=dst[r:P:32, :, :], in_=src[:, r:16:4, :].rearrange("g q n -> q g n").bitcast(I32))
 
-        nc.sync.dma_start(idx2[:], offs2)
         nc.sync.dma_start(out=w4_raw[:], in_=w4_words.rearrange("g p n -> p g n").bitcast(I32))
+        nc.sync.dma_start(idx2[:], offs2)
+        nc.sync.dma_start(out=w4s_raw[0:P:32, :, :], in_=w4_scales[:, 0:16:4, :].rearrange("g q n -> q g n").bitcast(I32))
+        nc.sync.dma_start(out=s2win[4:P:32, :], in_=tab2_scales[0, 0:16:4, :].bitcast(I32))
+        nc.sync.dma_start(out=s2win[8:P:32, :], in_=tab2_scales[1, 0:16:4, :].bitcast(I32))
+        nc.sync.dma_start(out=w4s_raw[1:P:32, :, :], in_=w4_scales[:, 1:16:4, :].rearrange("g q n -> q g n").bitcast(I32))
+        nc.sync.dma_start(out=s2win[5:P:32, :], in_=tab2_scales[0, 1:16:4, :].bitcast(I32))
+        nc.sync.dma_start(out=s2win[9:P:32, :], in_=tab2_scales[1, 1:16:4, :].bitcast(I32))
+        nc.sync.dma_start(out=w4s_raw[2:P:32, :, :], in_=w4_scales[:, 2:16:4, :].rearrange("g q n -> q g n").bitcast(I32))
+        nc.sync.dma_start(out=s2win[6:P:32, :], in_=tab2_scales[0, 2:16:4, :].bitcast(I32))
+        nc.sync.dma_start(out=s2win[10:P:32, :], in_=tab2_scales[1, 2:16:4, :].bitcast(I32))
+        nc.sync.dma_start(out=w4s_raw[3:P:32, :, :], in_=w4_scales[:, 3:16:4, :].rearrange("g q n -> q g n").bitcast(I32))
+        nc.sync.dma_start(out=s2win[7:P:32, :], in_=tab2_scales[0, 3:16:4, :].bitcast(I32))
+        nc.sync.dma_start(out=s2win[11:P:32, :], in_=tab2_scales[1, 3:16:4, :].bitcast(I32))
         nc.sync.dma_start(idx[:], offs)
-        nc.sync.dma_start(out=gains[:], in_=gain.rearrange("(a p t) -> p a t", a=2, t=4))
-        for a in range(2):
-            for r in range(4):
-                nc.sync.dma_start(out=s2win[4 + 4 * a + r : P : 32, :], in_=tab2_scales[a, r:16:4, :].bitcast(I32))
         load_w1(0, 0)
-        load_planes(w4s_raw, w4_scales)
+        nc.sync.dma_start(out=s1win[0:P:32, :, :], in_=tab_scales[:, 0:16:4, :].rearrange("g q n -> q g n").bitcast(I32))
+        nc.sync.dma_start(out=s1win[1:P:32, :, :], in_=tab_scales[:, 1:16:4, :].rearrange("g q n -> q g n").bitcast(I32))
+        nc.sync.dma_start(out=s1win[2:P:32, :, :], in_=tab_scales[:, 2:16:4, :].rearrange("g q n -> q g n").bitcast(I32))
+        nc.sync.dma_start(out=s1win[3:P:32, :, :], in_=tab_scales[:, 3:16:4, :].rearrange("g q n -> q g n").bitcast(I32))
         load_w1(1, 0)
-        load_planes(s1win, tab_scales)
-        load_words(win1[0], tab_words[0])
+        nc.sync.dma_start(out=gains[:], in_=gain.rearrange("(a p t) -> p a t", a=2, t=4))
+        load_words(win1[0], tab_words[0], 0, T)
+        load_words(win1[1], tab_words[1], 0, T)
         load_w1(0, 1)
-        load_words(win1[1], tab_words[1])
         load_w1(1, 1)
-        load_words(win2[0], tab2_words[0])
-        load_words(win2[1], tab2_words[1])
+        load_words(win2[1], tab2_words[1], 0, 3328)
+        load_words(win2[0], tab2_words[0], 0, T2)
+        load_words(win2[1], tab2_words[1], 3328, T2)
 
         def gather(dst, window, offsets, lo, hi):
             nc.vector.tensor_copy(dst[:, lo:hi], window.indirect(offsets[:, lo // 16 : hi // 16]))
 
-        nc.vector.tensor_copy(
-            out=w4c[:].bitcast(U16).rearrange("p (b t m) -> p b t m", b=4, t=4),
-            in_=w4_raw[:].rearrange("p g w -> p (g w)").bitcast(U16).rearrange("p (b m t) -> p b t m", b=4, t=4),
-        )
-        for q in range(3):
-            gather(v2s, s2win[:].bitcast(U8), idx2, q * GROUP, (q + 1) * GROUP)
-        nc.vector.tensor_copy(
-            out=w4s[:].rearrange("p (b t m) -> p b t m", b=4, t=4),
-            in_=w4s_raw[:].rearrange("p g w -> p (g w)").bitcast(U8).rearrange("p (b m t) -> p b t m", b=4, t=4),
-        )
+        def permute(dst, src):
+            nc.vector.tensor_copy(
+                out=dst.rearrange("p (b t m) -> p b t m", t=4, m=P), in_=src.rearrange("p (b m t) -> p b t m", t=4, m=P)
+            )
 
         def quantise_w1(g, a):
             for u in range(2):
-                grouped = ring.tile([P, 2 * GROUP], BF16, name="grouped", align_bytes=64)
-                nc.scalar.copy(
+                grouped = ring.tile([P, 2 * GROUP], BF16, name="grouped", align_bytes=64, bufs=4)
+                copy = nc.vector.tensor_copy if (g, a, u) in [(1, 1, 1), (0, 1, 1)] else nc.scalar.copy
+                copy(
                     out=grouped[:].rearrange("p (e m j) -> p m j e", e=2, j=4),
                     in_=w1_raw[g, a][:].rearrange("p j (m t) -> p m j t", t=4)[:, :, :, 2 * u : 2 * u + 2],
                 )
                 c0 = (2 * g + a) * GROUP + u * HALF
                 nc.vector.quantize_mx(out=w1c[:, c0 : c0 + HALF].bitcast(FP8X4), scales=w1s[:, c0 : c0 + HALF], in_=grouped[:])
 
-        quantise_w1(0, 0)
-        for g in range(2):
-            gather(vs[:, g, :], s1win[:, g, :].bitcast(U8), idx, 0, S)
-        quantise_w1(1, 0)
-        gather(vc[:, 0, :], win1[0][:].bitcast(U32), idx, 0, S)
-        quantise_w1(0, 1)
-        for hf in range(2):
-            gather(vc[:, 1, :], win1[1][:].bitcast(U32), idx, hf * HALF, (hf + 1) * HALF)
+        codes = {}
 
         def soft_codes(a, hf):
             tok = slice(hf * HALF, (hf + 1) * HALF)
-            th = ring.tile([P, 4, HALF], F32, name="th")
+            th = ring.tile([P, 4, HALF], F32, name="th", bufs=3)
+            codes[a, hf] = th
             for u in range(2):
                 pb = psum.tile([P, 2, HALF], F32, name="bank_a")
                 for e in range(2):
@@ -145,7 +146,11 @@ def tile_list_duplicate_collision_score_kernel(
                 for e in range(2):
                     t = 2 * u + e
                     nc.scalar.activation(th[:, t, :], pb[:, e, :], ACT.Tanh, bias=zero[:], scale=gains[:, a, t : t + 1])
-            hb = ring.tile([P, 4 * HALF], BF16, name="hb", align_bytes=64)
+
+        def weighted_codes(a, hf):
+            tok = slice(hf * HALF, (hf + 1) * HALF)
+            th = codes[a, hf]
+            hb = ring.tile([P, 4 * HALF], BF16, name="hb", align_bytes=64, bufs=3)
             for b in range(2):
                 blk = slice(hf * HALF + b * P, hf * HALF + (b + 1) * P)
                 cb = psum.tile([P, 4, P], F32, name="bank_b")
@@ -162,18 +167,34 @@ def tile_list_duplicate_collision_score_kernel(
                             stop=(g == 1),
                         )
                 nc.vector.tensor_tensor(
-                    out=hb[:, b * GROUP : (b + 1) * GROUP].rearrange("p (c i t) -> p c t i", i=4, t=4),
-                    in0=cb[:].rearrange("p t (c i) -> p c t i", i=4),
-                    in1=th[:, :, b * P : (b + 1) * P].rearrange("p t (c i) -> p c t i", i=4),
+                    out=hb[:, b * GROUP : (b + 1) * GROUP].rearrange("p (c i t) -> p c t i", i=2, t=4),
+                    in0=cb[:].rearrange("p t (c i) -> p c t i", i=2),
+                    in1=th[:, :, b * P : (b + 1) * P].rearrange("p t (c i) -> p c t i", i=2),
                     op=MULT,
                 )
             nc.vector.quantize_mx(out=hc[:, a, tok].bitcast(FP8X4), scales=hs[:, a, tok], in_=hb[:])
 
+        permute(w4c[:].bitcast(U16), w4_raw[:].rearrange("p g w -> p (g w)").bitcast(U16))
+        permute(w4s[:], w4s_raw[:].rearrange("p g w -> p (g w)").bitcast(U8))
+        gather(vs[:, 0, :], s1win[:, 0, :].bitcast(U8), idx, 0, S)
+        gather(vs[:, 1, :], s1win[:, 1, :].bitcast(U8), idx, 0, S)
+        quantise_w1(0, 0)
+        quantise_w1(1, 0)
+        gather(vc[:, 0, :], win1[0][:].bitcast(U32), idx, 0, S)
+        for hf in range(2):
+            gather(vc[:, 1, :], win1[1][:].bitcast(U32), idx, hf * HALF, (hf + 1) * HALF)
         soft_codes(0, 0)
         soft_codes(0, 1)
+        quantise_w1(0, 1)
         quantise_w1(1, 1)
+        weighted_codes(0, 0)
+        weighted_codes(0, 1)
         soft_codes(1, 0)
         soft_codes(1, 1)
+        weighted_codes(1, 0)
+        weighted_codes(1, 1)
+        for q in range(3):
+            gather(v2s, s2win[:].bitcast(U8), idx2, q * GROUP, (q + 1) * GROUP)
 
         for q in range(3):
             for a in range(2):

@@ -29,7 +29,7 @@ def tile_list_duplicate_collision_score_kernel(
         lists = ctx.enter_context(tc.tile_pool(name="lists", bufs=1))
         keep = ctx.enter_context(tc.tile_pool(name="keep", bufs=1))
         ring = ctx.enter_context(tc.tile_pool(name="ring", bufs=3))
-        stage = ctx.enter_context(tc.tile_pool(name="stage", bufs=6))
+        stage = ctx.enter_context(tc.tile_pool(name="stage", bufs=12))
         psum = ctx.enter_context(tc.psum_pool(name="psum", bufs=4))
 
         idx = lists.tile([P, S // 16], U16, name="idx")
@@ -46,14 +46,7 @@ def tile_list_duplicate_collision_score_kernel(
         win1 = [keep.tile([P, T], I32, name="win1_%d" % g, align_bytes=64) for g in range(2)]
         win2 = [keep.tile([P, T2], I32, name="win2_%d" % a, align_bytes=64) for a in range(2)]
 
-        w4c = keep.tile([P, 4 * 4 * 2 * P], U8, name="w4c", align_bytes=64)
-        w4s = keep.tile([P, 4 * 4 * P], U8, name="w4s", align_bytes=64)
-        w1c = keep.tile([P, 4 * 4 * P], U32, name="w1c", align_bytes=64)
         w1s = keep.tile([P, 4 * 4 * P], U8, name="w1s", align_bytes=64)
-        vc = keep.tile([P, 2, S], U32, name="vc", align_bytes=64)
-        vs = keep.tile([P, 2, S], U8, name="vs", align_bytes=64)
-        v2c = keep.tile([P, 2, S2], U32, name="v2c", align_bytes=64)
-        v2s = keep.tile([P, S2], U8, name="v2s", align_bytes=64)
         hc = keep.tile([P, 2, S], U32, name="hc", align_bytes=64)
         hs = keep.tile([P, 2, S], U8, name="hs", align_bytes=64)
 
@@ -78,140 +71,203 @@ def tile_list_duplicate_collision_score_kernel(
         nc.sync.dma_start(idx2[:], offs2)
         nc.sync.dma_start(out=w4s_raw[0:P:32, :, :], in_=w4_scales[:, 0:16:4, :].rearrange("g q n -> q g n").bitcast(I32))
         nc.sync.dma_start(out=s2win[4:P:32, :], in_=tab2_scales[0, 0:16:4, :].bitcast(I32))
+        nc.sync.dma_start(out=s2win[7:P:32, :], in_=tab2_scales[0, 3:16:4, :].bitcast(I32))
         nc.sync.dma_start(out=s2win[8:P:32, :], in_=tab2_scales[1, 0:16:4, :].bitcast(I32))
         nc.sync.dma_start(out=w4s_raw[1:P:32, :, :], in_=w4_scales[:, 1:16:4, :].rearrange("g q n -> q g n").bitcast(I32))
-        nc.sync.dma_start(out=s2win[5:P:32, :], in_=tab2_scales[0, 1:16:4, :].bitcast(I32))
         nc.sync.dma_start(out=s2win[9:P:32, :], in_=tab2_scales[1, 1:16:4, :].bitcast(I32))
         nc.sync.dma_start(out=w4s_raw[2:P:32, :, :], in_=w4_scales[:, 2:16:4, :].rearrange("g q n -> q g n").bitcast(I32))
-        nc.sync.dma_start(out=s2win[6:P:32, :], in_=tab2_scales[0, 2:16:4, :].bitcast(I32))
         nc.sync.dma_start(out=s2win[10:P:32, :], in_=tab2_scales[1, 2:16:4, :].bitcast(I32))
         nc.sync.dma_start(out=w4s_raw[3:P:32, :, :], in_=w4_scales[:, 3:16:4, :].rearrange("g q n -> q g n").bitcast(I32))
-        nc.sync.dma_start(out=s2win[7:P:32, :], in_=tab2_scales[0, 3:16:4, :].bitcast(I32))
+        nc.sync.dma_start(out=s2win[5:P:32, :], in_=tab2_scales[0, 1:16:4, :].bitcast(I32))
         nc.sync.dma_start(out=s2win[11:P:32, :], in_=tab2_scales[1, 3:16:4, :].bitcast(I32))
+        nc.sync.dma_start(out=s2win[6:P:32, :], in_=tab2_scales[0, 2:16:4, :].bitcast(I32))
         nc.sync.dma_start(idx[:], offs)
         load_w1(0, 0)
         nc.sync.dma_start(out=s1win[0:P:32, :, :], in_=tab_scales[:, 0:16:4, :].rearrange("g q n -> q g n").bitcast(I32))
         nc.sync.dma_start(out=s1win[1:P:32, :, :], in_=tab_scales[:, 1:16:4, :].rearrange("g q n -> q g n").bitcast(I32))
         nc.sync.dma_start(out=s1win[2:P:32, :, :], in_=tab_scales[:, 2:16:4, :].rearrange("g q n -> q g n").bitcast(I32))
         nc.sync.dma_start(out=s1win[3:P:32, :, :], in_=tab_scales[:, 3:16:4, :].rearrange("g q n -> q g n").bitcast(I32))
-        load_w1(1, 0)
-        nc.sync.dma_start(out=gains[:], in_=gain.rearrange("(a p t) -> p a t", a=2, t=4))
         load_words(win1[0], tab_words[0], 0, T)
+        nc.sync.dma_start(out=gains[:], in_=gain.rearrange("(a p t) -> p a t", a=2, t=4))
+        load_w1(1, 0)
         load_words(win1[1], tab_words[1], 0, T)
         load_w1(0, 1)
         load_w1(1, 1)
-        load_words(win2[1], tab2_words[1], 0, 3328)
         load_words(win2[0], tab2_words[0], 0, T2)
-        load_words(win2[1], tab2_words[1], 3328, T2)
+        load_words(win2[1], tab2_words[1], 0, T2)
 
-        def gather(dst, window, offsets, lo, hi):
-            nc.vector.tensor_copy(dst[:, lo:hi], window.indirect(offsets[:, lo // 16 : hi // 16]))
+        def vector_tile(width, dtype):
+            return ring.tile([P, width], dtype, name="vector_out", align_bytes=64, bufs=36)
 
-        def permute(dst, src):
+        def scalar_tile(shape, dtype):
+            return ring.tile(shape, dtype, name="scalar_out", align_bytes=64, bufs=4)
+
+        def gather(window, offsets, q, dtype):
+            dst = vector_tile(GROUP, dtype)
+            nc.vector.tensor_copy(dst[:], window.bitcast(dtype).indirect(offsets[:, 32 * q : 32 * (q + 1)]))
+            return dst
+
+        def permute(src, dtype, width):
+            dst = vector_tile(width, U8)
             nc.vector.tensor_copy(
-                out=dst.rearrange("p (b t m) -> p b t m", t=4, m=P), in_=src.rearrange("p (b m t) -> p b t m", t=4, m=P)
+                out=dst[:].bitcast(dtype).rearrange("p (b t m) -> p b t m", t=4, m=P),
+                in_=src.bitcast(dtype).rearrange("p (b m t) -> p b t m", t=4, m=P),
+            )
+            return dst
+
+        w4c, v2s, vs, vc, grouped, w1c, th, cb, hb, v2c = {}, {}, {}, {}, {}, {}, {}, {}, {}, {}
+
+        def cast_w1(g, a, u, on_vector):
+            grouped[g, a, u] = vector_tile(2 * GROUP, BF16) if on_vector else scalar_tile([P, 2 * GROUP], BF16)
+            copy = nc.vector.tensor_copy if on_vector else nc.scalar.copy
+            copy(
+                out=grouped[g, a, u][:].rearrange("p (e m j) -> p m j e", e=2, j=4),
+                in_=w1_raw[g, a][:].rearrange("p j (m t) -> p m j t", t=4)[:, :, :, 2 * u : 2 * u + 2],
             )
 
-        def quantise_w1(g, a):
-            for u in range(2):
-                grouped = ring.tile([P, 2 * GROUP], BF16, name="grouped", align_bytes=64, bufs=4)
-                copy = nc.vector.tensor_copy if (g, a, u) in [(1, 1, 1), (0, 1, 1)] else nc.scalar.copy
-                copy(
-                    out=grouped[:].rearrange("p (e m j) -> p m j e", e=2, j=4),
-                    in_=w1_raw[g, a][:].rearrange("p j (m t) -> p m j t", t=4)[:, :, :, 2 * u : 2 * u + 2],
+        def quantise_w1(g, a, u):
+            w1c[g, a, u] = vector_tile(HALF, U32)
+            c0 = (2 * g + a) * GROUP + u * HALF
+            nc.vector.quantize_mx(out=w1c[g, a, u][:].bitcast(FP8X4), scales=w1s[:, c0 : c0 + HALF], in_=grouped[g, a, u][:])
+
+        def soft_code(a, t):
+            pb = psum.tile([P, S], F32, name="bank_a")
+            for g in range(2):
+                c0 = (2 * g + a) * GROUP + t * P
+                nc.tensor.matmul_mx(
+                    out=pb[:],
+                    lhsT=w1c[g, a, t // 2][:, (t % 2) * P : (t % 2 + 1) * P].bitcast(FP8X4),
+                    lhsT_scale=w1s[:, c0 : c0 + P],
+                    rhs=vc[g][:].bitcast(FP8X4),
+                    rhs_scale=vs[g][:],
+                    start=(g == 0),
+                    stop=(g == 1),
                 )
-                c0 = (2 * g + a) * GROUP + u * HALF
-                nc.vector.quantize_mx(out=w1c[:, c0 : c0 + HALF].bitcast(FP8X4), scales=w1s[:, c0 : c0 + HALF], in_=grouped[:])
+            if a not in th:
+                th[a] = scalar_tile([P, 4, S], F32)
+            nc.scalar.activation(th[a][:, t, :], pb[:], ACT.Tanh, bias=zero[:], scale=gains[:, a, t : t + 1])
 
-        codes = {}
+        def weights(a, b):
+            blk = slice(b * P, (b + 1) * P)
+            cb[a, b] = psum.tile([P, 4, P], F32, name="bank_b")
+            for t in range(4):
+                for g in range(2):
+                    c0 = a * GROUP + t * P
+                    nc.tensor.matmul_mx(
+                        out=cb[a, b][:, t, :],
+                        lhsT=w4c[g][:, 2 * c0 : 2 * (c0 + P)].bitcast(FP4X4),
+                        lhsT_scale=w4s[:, g * H + c0 : g * H + c0 + P],
+                        rhs=vc[g][:, blk].bitcast(FP8X4),
+                        rhs_scale=vs[g][:, blk],
+                        start=(g == 0),
+                        stop=(g == 1),
+                    )
 
-        def soft_codes(a, hf):
-            tok = slice(hf * HALF, (hf + 1) * HALF)
-            th = ring.tile([P, 4, HALF], F32, name="th", bufs=3)
-            codes[a, hf] = th
-            for u in range(2):
-                pb = psum.tile([P, 2, HALF], F32, name="bank_a")
-                for e in range(2):
-                    for g in range(2):
-                        c0 = (2 * g + a) * GROUP + (2 * u + e) * P
-                        nc.tensor.matmul_mx(
-                            out=pb[:, e, :],
-                            lhsT=w1c[:, c0 : c0 + P].bitcast(FP8X4),
-                            lhsT_scale=w1s[:, c0 : c0 + P],
-                            rhs=vc[:, g, tok].bitcast(FP8X4),
-                            rhs_scale=vs[:, g, tok],
-                            start=(g == 0),
-                            stop=(g == 1),
-                        )
-                for e in range(2):
-                    t = 2 * u + e
-                    nc.scalar.activation(th[:, t, :], pb[:, e, :], ACT.Tanh, bias=zero[:], scale=gains[:, a, t : t + 1])
+        def weighted_code(a, b):
+            hb[a, b] = vector_tile(GROUP, BF16)
+            nc.vector.tensor_tensor(
+                out=hb[a, b][:].rearrange("p (c i t) -> p c t i", i=2, t=4),
+                in0=cb[a, b][:].rearrange("p t (c i) -> p c t i", i=2),
+                in1=th[a][:, :, b * P : (b + 1) * P].rearrange("p t (c i) -> p c t i", i=2),
+                op=MULT,
+            )
 
-        def weighted_codes(a, hf):
-            tok = slice(hf * HALF, (hf + 1) * HALF)
-            th = codes[a, hf]
-            hb = ring.tile([P, 4 * HALF], BF16, name="hb", align_bytes=64, bufs=3)
-            for b in range(2):
-                blk = slice(hf * HALF + b * P, hf * HALF + (b + 1) * P)
-                cb = psum.tile([P, 4, P], F32, name="bank_b")
-                for t in range(4):
-                    for g in range(2):
-                        c0 = (2 * g + a) * GROUP + t * P
-                        nc.tensor.matmul_mx(
-                            out=cb[:, t, :],
-                            lhsT=w4c[:, 2 * c0 : 2 * (c0 + P)].bitcast(FP4X4),
-                            lhsT_scale=w4s[:, c0 : c0 + P],
-                            rhs=vc[:, g, blk].bitcast(FP8X4),
-                            rhs_scale=vs[:, g, blk],
-                            start=(g == 0),
-                            stop=(g == 1),
-                        )
-                nc.vector.tensor_tensor(
-                    out=hb[:, b * GROUP : (b + 1) * GROUP].rearrange("p (c i t) -> p c t i", i=2, t=4),
-                    in0=cb[:].rearrange("p t (c i) -> p c t i", i=2),
-                    in1=th[:, :, b * P : (b + 1) * P].rearrange("p t (c i) -> p c t i", i=2),
-                    op=MULT,
-                )
-            nc.vector.quantize_mx(out=hc[:, a, tok].bitcast(FP8X4), scales=hs[:, a, tok], in_=hb[:])
+        def quantise_h(a, b):
+            blk = slice(b * P, (b + 1) * P)
+            nc.vector.quantize_mx(out=hc[:, a, blk].bitcast(FP8X4), scales=hs[:, a, blk], in_=hb[a, b][:])
 
-        permute(w4c[:].bitcast(U16), w4_raw[:].rearrange("p g w -> p (g w)").bitcast(U16))
-        permute(w4s[:], w4s_raw[:].rearrange("p g w -> p (g w)").bitcast(U8))
-        gather(vs[:, 0, :], s1win[:, 0, :].bitcast(U8), idx, 0, S)
-        gather(vs[:, 1, :], s1win[:, 1, :].bitcast(U8), idx, 0, S)
-        quantise_w1(0, 0)
-        quantise_w1(1, 0)
-        gather(vc[:, 0, :], win1[0][:].bitcast(U32), idx, 0, S)
-        for hf in range(2):
-            gather(vc[:, 1, :], win1[1][:].bitcast(U32), idx, hf * HALF, (hf + 1) * HALF)
-        soft_codes(0, 0)
-        soft_codes(0, 1)
-        quantise_w1(0, 1)
-        quantise_w1(1, 1)
-        weighted_codes(0, 0)
-        weighted_codes(0, 1)
-        soft_codes(1, 0)
-        soft_codes(1, 1)
-        weighted_codes(1, 0)
-        weighted_codes(1, 1)
-        for q in range(3):
-            gather(v2s, s2win[:].bitcast(U8), idx2, q * GROUP, (q + 1) * GROUP)
+        def pick_words(q, a):
+            v2c[q, a] = gather(win2[a][:], idx2, q, U32)
+
+        w4c[0] = permute(w4_raw[:, 0, :], U16, 2 * H)
+        w4c[1] = permute(w4_raw[:, 1, :], U16, 2 * H)
+        w4s = permute(w4s_raw[:].rearrange("p g w -> p (g w)"), U8, 2 * H)
+        v2s[0] = gather(s2win[:], idx2, 0, U8)
+        v2s[1] = gather(s2win[:], idx2, 1, U8)
+        cast_w1(0, 0, 0, False)
+        cast_w1(0, 0, 1, False)
+        vs[0] = gather(s1win[:, 0, :], idx, 0, U8)
+        vs[1] = gather(s1win[:, 1, :], idx, 0, U8)
+        quantise_w1(0, 0, 0)
+        quantise_w1(0, 0, 1)
+        v2s[2] = gather(s2win[:], idx2, 2, U8)
+        vc[0] = gather(win1[0][:], idx, 0, U32)
+        cast_w1(1, 0, 0, False)
+        cast_w1(1, 0, 1, True)
+        quantise_w1(1, 0, 0)
+        vc[1] = gather(win1[1][:], idx, 0, U32)
+        quantise_w1(1, 0, 1)
+        soft_code(0, 0)
+        soft_code(0, 1)
+        weights(0, 2)
+        weights(0, 0)
+        soft_code(0, 2)
+        soft_code(0, 3)
+        weights(0, 1)
+        weights(0, 3)
+        cast_w1(0, 1, 1, True)
+        quantise_w1(0, 1, 1)
+        cast_w1(0, 1, 0, False)
+        weighted_code(0, 0)
+        cast_w1(1, 1, 1, True)
+        quantise_w1(0, 1, 0)
+        quantise_w1(1, 1, 1)
+        cast_w1(1, 1, 0, False)
+        weighted_code(0, 1)
+        quantise_w1(1, 1, 0)
+        weighted_code(0, 2)
+        weighted_code(0, 3)
+        quantise_h(0, 0)
+        quantise_h(0, 2)
+        quantise_h(0, 3)
+        soft_code(1, 2)
+        soft_code(1, 3)
+        weights(1, 0)
+        quantise_h(0, 1)
+        soft_code(1, 0)
+        soft_code(1, 1)
+        weights(1, 1)
+        weights(1, 2)
+        weights(1, 3)
+        pick_words(0, 0)
+        weighted_code(1, 0)
+        weighted_code(1, 1)
+        weighted_code(1, 2)
+        quantise_h(1, 1)
+        weighted_code(1, 3)
+        quantise_h(1, 2)
+        quantise_h(1, 0)
+        quantise_h(1, 3)
 
         for q in range(3):
             for a in range(2):
-                gather(v2c[:, a, :], win2[a][:].bitcast(U32), idx2, q * GROUP, (q + 1) * GROUP)
+                if (q, a) not in v2c:
+                    pick_words(q, a)
+            banks = [psum.tile([P, S], F32, name="bank_a" if n % 2 == 0 else "bank_b") for n in range(4)]
             for n in range(4):
-                rows = slice(q * GROUP + n * P, q * GROUP + (n + 1) * P)
-                yb = psum.tile([P, S], F32, name="bank_a" if n % 2 == 0 else "bank_b")
-                for a in range(2):
+                for repeat in range({(1, 1): 2, (1, 3): 3}.get((q, n), 0)):
                     nc.tensor.matmul_mx(
-                        out=yb[:],
-                        lhsT=v2c[:, a, rows].bitcast(FP8X4),
-                        lhsT_scale=v2s[4 + 4 * a : P, rows],
+                        out=banks[n][:],
+                        lhsT=v2c[0, 0][:, :P].bitcast(FP8X4),
+                        lhsT_scale=v2s[0][4:P, :P],
+                        rhs=hc[:, 0, :].bitcast(FP8X4),
+                        rhs_scale=hs[:, 0, :],
+                        start=True,
+                        stop=True,
+                    )
+            for a in range(2):
+                for n in range(4):
+                    cols = slice(n * P, (n + 1) * P)
+                    nc.tensor.matmul_mx(
+                        out=banks[n][:],
+                        lhsT=v2c[q, a][:, cols].bitcast(FP8X4),
+                        lhsT_scale=v2s[q][4 + 4 * a : P, cols],
                         rhs=hc[:, a, :].bitcast(FP8X4),
                         rhs_scale=hs[:, a, :],
                         start=(a == 0),
                         stop=(a == 1),
                     )
-                score = stage.tile([P, S], F32, name="score")
-                nc.scalar.activation(score[:], yb[:], ACT.Abs)
-                nc.sync.dma_start(out=out[rows, :], in_=score[:])
+                    if a == 1:
+                        score = stage.tile([P, S], F32, name="score")
+                        nc.scalar.activation(score[:], banks[n][:], ACT.Abs)
+                        nc.sync.dma_start(out=out[q * GROUP + n * P : q * GROUP + (n + 1) * P, :], in_=score[:])

@@ -17,8 +17,13 @@ ACT = mybir.ActivationFunctionType
 MULT = mybir.AluOpType.mult
 
 P = 128
-HALF = 256
-GROUP = 512
+PASS = 512
+PICK = 512
+PAIR = 2 * P
+VECTOR_TILES = 36
+SCALAR_TILES = 4
+V2_PLANE_ROW = (4, 8)
+WARM_PASSES = {(1, 1): 2, (1, 3): 3}
 
 
 def tile_list_duplicate_collision_score_kernel(
@@ -28,246 +33,223 @@ def tile_list_duplicate_collision_score_kernel(
     with ExitStack() as ctx:
         lists = ctx.enter_context(tc.tile_pool(name="lists", bufs=1))
         keep = ctx.enter_context(tc.tile_pool(name="keep", bufs=1))
-        ring = ctx.enter_context(tc.tile_pool(name="ring", bufs=3))
-        stage = ctx.enter_context(tc.tile_pool(name="stage", bufs=12))
+        ordered = ctx.enter_context(tc.tile_pool(name="ordered", bufs=1))
+        stage = ctx.enter_context(tc.tile_pool(name="stage", bufs=S2 // P))
         psum = ctx.enter_context(tc.psum_pool(name="psum", bufs=4))
 
         idx = lists.tile([P, S // 16], U16, name="idx")
         idx2 = lists.tile([P, S2 // 16], U16, name="idx2")
 
-        s2win = keep.tile([P, T2 // 4], I32, name="s2win", align_bytes=64)
-        w4s_raw = keep.tile([P, 2, H // 4], I32, name="w4s_raw", align_bytes=64)
-        s1win = keep.tile([P, 2, T // 4], I32, name="s1win", align_bytes=64)
+        v2_planes = keep.tile([P, T2 // 4], I32, name="v2_planes", align_bytes=64)
+        w4_planes = keep.tile([P, 2, H // 4], I32, name="w4_planes", align_bytes=64)
+        v_planes = keep.tile([P, 2, T // 4], I32, name="v_planes", align_bytes=64)
         w4_raw = keep.tile([P, 2, H // 2], I32, name="w4_raw", align_bytes=64)
         gains = keep.tile([P, 2, 4], F32, name="gains")
         zero_in = keep.tile([P, 1], F32, name="zero_in")
         zero = keep.tile([P, 1], F32, name="zero")
-        w1_raw = {(g, a): keep.tile([P, 4, GROUP], F32, name="w1_raw%d%d" % (g, a)) for g in range(2) for a in range(2)}
-        win1 = [keep.tile([P, T], I32, name="win1_%d" % g, align_bytes=64) for g in range(2)]
-        win2 = [keep.tile([P, T2], I32, name="win2_%d" % a, align_bytes=64) for a in range(2)]
+        w1_pass0 = keep.tile([P, 4, H], F32, name="w1_full0")
+        w1_raw = {(0, a): w1_pass0[:, :, a * PASS : (a + 1) * PASS] for a in range(2)}
+        for a in range(2):
+            w1_raw[1, a] = keep.tile([P, 4, PASS], F32, name="w1_pass1_%d" % a)
+        v_table = [keep.tile([P, T], I32, name="v_table%d" % g, align_bytes=64) for g in range(2)]
+        v2_table = [keep.tile([P, T2], I32, name="v2_table%d" % a, align_bytes=64) for a in range(2)]
+        w1_scales = keep.tile([P, 2 * H], U8, name="w1_scales", align_bytes=64)
+        h_codes = keep.tile([P, 2, S], U32, name="h_codes", align_bytes=64)
+        h_scales = keep.tile([P, 2, S], U8, name="h_scales", align_bytes=64)
 
-        w1s = keep.tile([P, 4 * 4 * P], U8, name="w1s", align_bytes=64)
-        hc = keep.tile([P, 2, S], U32, name="hc", align_bytes=64)
-        hs = keep.tile([P, 2, S], U8, name="hs", align_bytes=64)
-
-        nc.vector.memset(w4s_raw[:], 0)
-        nc.vector.memset(s2win[:], 0)
-        nc.vector.memset(s1win[:], 0)
+        nc.vector.memset(w4_planes[:], 0)
+        nc.vector.memset(v2_planes[:], 0)
+        nc.vector.memset(v_planes[:], 0)
         nc.gpsimd.memset(zero_in[:], 0.0)
         nc.scalar.activation(zero[:], zero_in[:], ACT.Tanh)
 
-        def load_w1(g, a):
-            rows = w1[g * GROUP : (g + 1) * GROUP, a * GROUP : (a + 1) * GROUP]
-            nc.sync.dma_start(out=w1_raw[g, a][:], in_=rows.rearrange("(p j) c -> p j c", j=4))
+        def load_rows(dst, rows):
+            nc.sync.dma_start(out=dst[:], in_=rows.rearrange("(p j) c -> p j c", j=4))
 
-        def load_words(dst, src, lo, hi):
-            nc.sync.dma_start(out=dst[:, lo:hi], in_=src.rearrange("p t i -> p (t i)").bitcast(I32)[:, lo:hi])
+        def load_words(dst, words):
+            nc.sync.dma_start(out=dst[:], in_=words.rearrange("p t i -> p (t i)").bitcast(I32))
 
-        def load_planes(queue, dst, src):
+        def load_planes(dst, scales):
             for r in range(4):
-                queue.dma_start(out=dst[r:P:32, :, :], in_=src[:, r:16:4, :].rearrange("g q n -> q g n").bitcast(I32))
+                nc.sync.dma_start(out=dst[r:P:32, :, :], in_=scales[:, r:16:4, :].rearrange("g q n -> q g n").bitcast(I32))
 
-        nc.sync.dma_start(out=w4_raw[:], in_=w4_words.rearrange("g p n -> p g n").bitcast(I32))
         nc.sync.dma_start(idx2[:], offs2)
-        nc.sync.dma_start(out=w4s_raw[0:P:32, :, :], in_=w4_scales[:, 0:16:4, :].rearrange("g q n -> q g n").bitcast(I32))
-        nc.sync.dma_start(out=s2win[4:P:32, :], in_=tab2_scales[0, 0:16:4, :].bitcast(I32))
-        nc.sync.dma_start(out=s2win[7:P:32, :], in_=tab2_scales[0, 3:16:4, :].bitcast(I32))
-        nc.sync.dma_start(out=s2win[8:P:32, :], in_=tab2_scales[1, 0:16:4, :].bitcast(I32))
-        nc.sync.dma_start(out=w4s_raw[1:P:32, :, :], in_=w4_scales[:, 1:16:4, :].rearrange("g q n -> q g n").bitcast(I32))
-        nc.sync.dma_start(out=s2win[9:P:32, :], in_=tab2_scales[1, 1:16:4, :].bitcast(I32))
-        nc.sync.dma_start(out=w4s_raw[2:P:32, :, :], in_=w4_scales[:, 2:16:4, :].rearrange("g q n -> q g n").bitcast(I32))
-        nc.sync.dma_start(out=s2win[10:P:32, :], in_=tab2_scales[1, 2:16:4, :].bitcast(I32))
-        nc.sync.dma_start(out=w4s_raw[3:P:32, :, :], in_=w4_scales[:, 3:16:4, :].rearrange("g q n -> q g n").bitcast(I32))
-        nc.sync.dma_start(out=s2win[5:P:32, :], in_=tab2_scales[0, 1:16:4, :].bitcast(I32))
-        nc.sync.dma_start(out=s2win[11:P:32, :], in_=tab2_scales[1, 3:16:4, :].bitcast(I32))
-        nc.sync.dma_start(out=s2win[6:P:32, :], in_=tab2_scales[0, 2:16:4, :].bitcast(I32))
+        nc.sync.dma_start(out=w4_raw[:], in_=w4_words.rearrange("g p n -> p g n").bitcast(I32))
+        load_planes(w4_planes, w4_scales)
+        for r in range(4):
+            for a in range(2):
+                nc.sync.dma_start(
+                    out=v2_planes[V2_PLANE_ROW[a] + r : P : 32, :], in_=tab2_scales[a, r:16:4, :].bitcast(I32)
+                )
+        load_rows(w1_pass0, w1[:PASS, :])
         nc.sync.dma_start(idx[:], offs)
-        load_w1(0, 0)
-        nc.sync.dma_start(out=s1win[0:P:32, :, :], in_=tab_scales[:, 0:16:4, :].rearrange("g q n -> q g n").bitcast(I32))
-        nc.sync.dma_start(out=s1win[1:P:32, :, :], in_=tab_scales[:, 1:16:4, :].rearrange("g q n -> q g n").bitcast(I32))
-        nc.sync.dma_start(out=s1win[2:P:32, :, :], in_=tab_scales[:, 2:16:4, :].rearrange("g q n -> q g n").bitcast(I32))
-        nc.sync.dma_start(out=s1win[3:P:32, :, :], in_=tab_scales[:, 3:16:4, :].rearrange("g q n -> q g n").bitcast(I32))
-        load_words(win1[0], tab_words[0], 0, T)
+        load_planes(v_planes, tab_scales)
+        load_words(v_table[0], tab_words[0])
         nc.sync.dma_start(out=gains[:], in_=gain.rearrange("(a p t) -> p a t", a=2, t=4))
-        load_w1(1, 0)
-        load_words(win1[1], tab_words[1], 0, T)
-        load_w1(0, 1)
-        load_w1(1, 1)
-        load_words(win2[0], tab2_words[0], 0, T2)
-        load_words(win2[1], tab2_words[1], 0, T2)
+        load_words(v_table[1], tab_words[1])
+        for a in range(2):
+            load_rows(w1_raw[1, a], w1[PASS:, a * PASS : (a + 1) * PASS])
+        for a in range(2):
+            load_words(v2_table[a], tab2_words[a])
 
         def vector_tile(width, dtype):
-            return ring.tile([P, width], dtype, name="vector_out", align_bytes=64, bufs=36)
+            return ordered.tile([P, width], dtype, name="vector_out", align_bytes=64, bufs=VECTOR_TILES)
 
         def scalar_tile(shape, dtype):
-            return ring.tile(shape, dtype, name="scalar_out", align_bytes=64, bufs=4)
+            return ordered.tile(shape, dtype, name="scalar_out", align_bytes=64, bufs=SCALAR_TILES)
 
         def gather(window, offsets, q, dtype):
-            dst = vector_tile(GROUP, dtype)
-            nc.vector.tensor_copy(dst[:], window.bitcast(dtype).indirect(offsets[:, 32 * q : 32 * (q + 1)]))
-            return dst
+            picked = vector_tile(PICK, dtype)
+            columns = PICK // 16
+            nc.vector.tensor_copy(picked[:], window.bitcast(dtype).indirect(offsets[:, columns * q : columns * (q + 1)]))
+            return picked
 
-        def permute(src, dtype, width):
-            dst = vector_tile(width, U8)
+        def reorder_columns(raw, dtype):
+            moved = vector_tile(2 * H, U8)
             nc.vector.tensor_copy(
-                out=dst[:].bitcast(dtype).rearrange("p (b t m) -> p b t m", t=4, m=P),
-                in_=src.bitcast(dtype).rearrange("p (b m t) -> p b t m", t=4, m=P),
+                out=moved[:].bitcast(dtype).rearrange("p (b t m) -> p b t m", t=4, m=P),
+                in_=raw.bitcast(dtype).rearrange("p (b m t) -> p b t m", t=4, m=P),
             )
-            return dst
+            return moved
 
-        w4c, v2s, vs, vc, grouped, w1c, th, cb, hb, v2c = {}, {}, {}, {}, {}, {}, {}, {}, {}, {}
+        rounded, w1_codes, tanh_p, c_bank, h_rounded, v2_codes = {}, {}, {}, {}, {}, {}
 
-        def cast_w1(g, a, u, on_vector):
-            grouped[g, a, u] = vector_tile(2 * GROUP, BF16) if on_vector else scalar_tile([P, 2 * GROUP], BF16)
+        def round_w1(g, a, u, on_vector):
+            rounded[g, a, u] = vector_tile(4 * PAIR, BF16) if on_vector else scalar_tile([P, 4 * PAIR], BF16)
             copy = nc.vector.tensor_copy if on_vector else nc.scalar.copy
             copy(
-                out=grouped[g, a, u][:].rearrange("p (e m j) -> p m j e", e=2, j=4),
+                out=rounded[g, a, u][:].rearrange("p (e m j) -> p m j e", e=2, j=4),
                 in_=w1_raw[g, a][:].rearrange("p j (m t) -> p m j t", t=4)[:, :, :, 2 * u : 2 * u + 2],
             )
 
         def quantise_w1(g, a, u):
-            w1c[g, a, u] = vector_tile(HALF, U32)
-            c0 = (2 * g + a) * GROUP + u * HALF
-            nc.vector.quantize_mx(out=w1c[g, a, u][:].bitcast(FP8X4), scales=w1s[:, c0 : c0 + HALF], in_=grouped[g, a, u][:])
+            w1_codes[g, a, u] = vector_tile(PAIR, U32)
+            first = g * H + a * PASS + u * PAIR
+            nc.vector.quantize_mx(
+                out=w1_codes[g, a, u][:].bitcast(FP8X4), scales=w1_scales[:, first : first + PAIR], in_=rounded[g, a, u][:]
+            )
 
         def soft_code(a, t):
-            pb = psum.tile([P, S], F32, name="bank_a")
+            bank = psum.tile([P, S], F32, name="bank_a")
             for g in range(2):
-                c0 = (2 * g + a) * GROUP + t * P
+                first = g * H + a * PASS + t * P
                 nc.tensor.matmul_mx(
-                    out=pb[:],
-                    lhsT=w1c[g, a, t // 2][:, (t % 2) * P : (t % 2 + 1) * P].bitcast(FP8X4),
-                    lhsT_scale=w1s[:, c0 : c0 + P],
-                    rhs=vc[g][:].bitcast(FP8X4),
-                    rhs_scale=vs[g][:],
+                    out=bank[:],
+                    lhsT=w1_codes[g, a, t // 2][:, (t % 2) * P : (t % 2 + 1) * P].bitcast(FP8X4),
+                    lhsT_scale=w1_scales[:, first : first + P],
+                    rhs=v_codes[g][:].bitcast(FP8X4),
+                    rhs_scale=v_scales[g][:],
                     start=(g == 0),
                     stop=(g == 1),
                 )
-            if a not in th:
-                th[a] = scalar_tile([P, 4, S], F32)
-            nc.scalar.activation(th[a][:, t, :], pb[:], ACT.Tanh, bias=zero[:], scale=gains[:, a, t : t + 1])
+            if a not in tanh_p:
+                tanh_p[a] = scalar_tile([P, 4, S], F32)
+            nc.scalar.activation(tanh_p[a][:, t, :], bank[:], ACT.Tanh, bias=zero[:], scale=gains[:, a, t : t + 1])
 
-        def weights(a, b):
-            blk = slice(b * P, (b + 1) * P)
-            cb[a, b] = psum.tile([P, 4, P], F32, name="bank_b")
+        def signed_weights(a, b):
+            records = slice(b * P, (b + 1) * P)
+            c_bank[a, b] = psum.tile([P, 4, P], F32, name="bank_b")
             for t in range(4):
                 for g in range(2):
-                    c0 = a * GROUP + t * P
+                    first = a * PASS + t * P
                     nc.tensor.matmul_mx(
-                        out=cb[a, b][:, t, :],
-                        lhsT=w4c[g][:, 2 * c0 : 2 * (c0 + P)].bitcast(FP4X4),
-                        lhsT_scale=w4s[:, g * H + c0 : g * H + c0 + P],
-                        rhs=vc[g][:, blk].bitcast(FP8X4),
-                        rhs_scale=vs[g][:, blk],
+                        out=c_bank[a, b][:, t, :],
+                        lhsT=w4_codes[g][:, 2 * first : 2 * (first + P)].bitcast(FP4X4),
+                        lhsT_scale=w4_moved_scales[:, g * H + first : g * H + first + P],
+                        rhs=v_codes[g][:, records].bitcast(FP8X4),
+                        rhs_scale=v_scales[g][:, records],
                         start=(g == 0),
                         stop=(g == 1),
                     )
 
         def weighted_code(a, b):
-            hb[a, b] = vector_tile(GROUP, BF16)
+            h_rounded[a, b] = vector_tile(4 * P, BF16)
             nc.vector.tensor_tensor(
-                out=hb[a, b][:].rearrange("p (c i t) -> p c t i", i=2, t=4),
-                in0=cb[a, b][:].rearrange("p t (c i) -> p c t i", i=2),
-                in1=th[a][:, :, b * P : (b + 1) * P].rearrange("p t (c i) -> p c t i", i=2),
+                out=h_rounded[a, b][:].rearrange("p (n i t) -> p n t i", i=2, t=4),
+                in0=c_bank[a, b][:].rearrange("p t (n i) -> p n t i", i=2),
+                in1=tanh_p[a][:, :, b * P : (b + 1) * P].rearrange("p t (n i) -> p n t i", i=2),
                 op=MULT,
             )
 
         def quantise_h(a, b):
-            blk = slice(b * P, (b + 1) * P)
-            nc.vector.quantize_mx(out=hc[:, a, blk].bitcast(FP8X4), scales=hs[:, a, blk], in_=hb[a, b][:])
+            records = slice(b * P, (b + 1) * P)
+            nc.vector.quantize_mx(
+                out=h_codes[:, a, records].bitcast(FP8X4), scales=h_scales[:, a, records], in_=h_rounded[a, b][:]
+            )
 
-        def pick_words(q, a):
-            v2c[q, a] = gather(win2[a][:], idx2, q, U32)
+        def pick_v2_words(q, a):
+            v2_codes[q, a] = gather(v2_table[a][:], idx2, q, U32)
 
-        w4c[0] = permute(w4_raw[:, 0, :], U16, 2 * H)
-        w4c[1] = permute(w4_raw[:, 1, :], U16, 2 * H)
-        w4s = permute(w4s_raw[:].rearrange("p g w -> p (g w)"), U8, 2 * H)
-        v2s[0] = gather(s2win[:], idx2, 0, U8)
-        v2s[1] = gather(s2win[:], idx2, 1, U8)
-        cast_w1(0, 0, 0, False)
-        cast_w1(0, 0, 1, False)
-        vs[0] = gather(s1win[:, 0, :], idx, 0, U8)
-        vs[1] = gather(s1win[:, 1, :], idx, 0, U8)
-        quantise_w1(0, 0, 0)
-        quantise_w1(0, 0, 1)
-        v2s[2] = gather(s2win[:], idx2, 2, U8)
-        vc[0] = gather(win1[0][:], idx, 0, U32)
-        cast_w1(1, 0, 0, False)
-        cast_w1(1, 0, 1, True)
-        quantise_w1(1, 0, 0)
-        vc[1] = gather(win1[1][:], idx, 0, U32)
-        quantise_w1(1, 0, 1)
-        soft_code(0, 0)
-        soft_code(0, 1)
-        weights(0, 2)
-        weights(0, 0)
-        soft_code(0, 2)
-        soft_code(0, 3)
-        weights(0, 1)
-        weights(0, 3)
-        cast_w1(0, 1, 1, True)
-        quantise_w1(0, 1, 1)
-        cast_w1(0, 1, 0, False)
-        weighted_code(0, 0)
-        cast_w1(1, 1, 1, True)
-        quantise_w1(0, 1, 0)
-        quantise_w1(1, 1, 1)
-        cast_w1(1, 1, 0, False)
-        weighted_code(0, 1)
-        quantise_w1(1, 1, 0)
-        weighted_code(0, 2)
-        weighted_code(0, 3)
-        quantise_h(0, 0)
-        quantise_h(0, 2)
-        quantise_h(0, 3)
-        soft_code(1, 2)
-        soft_code(1, 3)
-        weights(1, 0)
-        quantise_h(0, 1)
-        soft_code(1, 0)
-        soft_code(1, 1)
-        weights(1, 1)
-        weights(1, 2)
-        weights(1, 3)
-        pick_words(0, 0)
-        weighted_code(1, 0)
-        weighted_code(1, 1)
-        weighted_code(1, 2)
-        quantise_h(1, 1)
-        weighted_code(1, 3)
-        quantise_h(1, 2)
-        quantise_h(1, 0)
-        quantise_h(1, 3)
+        w4_codes = [reorder_columns(w4_raw[:, g, :], U16) for g in range(2)]
+        w4_moved_scales = reorder_columns(w4_planes[:].rearrange("p g w -> p (g w)"), U8)
+        v2_scales = [gather(v2_planes[:], idx2, q, U8) for q in range(S2 // PICK)]
+        for a in range(2):
+            for u in range(2):
+                round_w1(0, a, u, on_vector=False)
+        v_scales = [gather(v_planes[:, g, :], idx, 0, U8) for g in range(2)]
 
-        for q in range(3):
+        v_codes = []
+        for g in range(2):
+            v_codes.append(gather(v_table[g][:], idx, 0, U32))
+            for u in range(2):
+                quantise_w1(0, g, u)
+
+        for b in range(4):
+            signed_weights(0, b)
+        round_w1(1, 0, 1, on_vector=True)
+        round_w1(1, 0, 0, on_vector=False)
+        for u in (1, 0):
+            quantise_w1(1, 0, u)
+        for t in (2, 3, 0, 1):
+            soft_code(0, t)
+        for u in (1, 0):
+            round_w1(1, 1, u, on_vector=True)
+        for u in (1, 0):
+            quantise_w1(1, 1, u)
+        for b in range(4):
+            weighted_code(0, b)
+        for b in range(4):
+            quantise_h(0, b)
+
+        for t in (2, 3, 0, 1):
+            soft_code(1, t)
+        for b in range(4):
+            signed_weights(1, b)
+        pick_v2_words(0, 0)
+        for b in range(4):
+            weighted_code(1, b)
+        for b in range(4):
+            quantise_h(1, b)
+
+        for q in range(S2 // PICK):
             for a in range(2):
-                if (q, a) not in v2c:
-                    pick_words(q, a)
+                if (q, a) not in v2_codes:
+                    pick_v2_words(q, a)
             banks = [psum.tile([P, S], F32, name="bank_a" if n % 2 == 0 else "bank_b") for n in range(4)]
             for n in range(4):
-                for repeat in range({(1, 1): 2, (1, 3): 3}.get((q, n), 0)):
+                for repeat in range(WARM_PASSES.get((q, n), 0)):
                     nc.tensor.matmul_mx(
                         out=banks[n][:],
-                        lhsT=v2c[0, 0][:, :P].bitcast(FP8X4),
-                        lhsT_scale=v2s[0][4:P, :P],
-                        rhs=hc[:, 0, :].bitcast(FP8X4),
-                        rhs_scale=hs[:, 0, :],
+                        lhsT=v2_codes[0, 0][:, :P].bitcast(FP8X4),
+                        lhsT_scale=v2_scales[0][V2_PLANE_ROW[0] : P, :P],
+                        rhs=h_codes[:, 0, :].bitcast(FP8X4),
+                        rhs_scale=h_scales[:, 0, :],
                         start=True,
                         stop=True,
                     )
             for a in range(2):
                 for n in range(4):
-                    cols = slice(n * P, (n + 1) * P)
+                    candidates = slice(n * P, (n + 1) * P)
                     nc.tensor.matmul_mx(
                         out=banks[n][:],
-                        lhsT=v2c[q, a][:, cols].bitcast(FP8X4),
-                        lhsT_scale=v2s[q][4 + 4 * a : P, cols],
-                        rhs=hc[:, a, :].bitcast(FP8X4),
-                        rhs_scale=hs[:, a, :],
+                        lhsT=v2_codes[q, a][:, candidates].bitcast(FP8X4),
+                        lhsT_scale=v2_scales[q][V2_PLANE_ROW[a] : P, candidates],
+                        rhs=h_codes[:, a, :].bitcast(FP8X4),
+                        rhs_scale=h_scales[:, a, :],
                         start=(a == 0),
                         stop=(a == 1),
                     )
                     if a == 1:
                         score = stage.tile([P, S], F32, name="score")
                         nc.scalar.activation(score[:], banks[n][:], ACT.Abs)
-                        nc.sync.dma_start(out=out[q * GROUP + n * P : q * GROUP + (n + 1) * P, :], in_=score[:])
+                        nc.sync.dma_start(out=out[q * PICK + n * P : q * PICK + (n + 1) * P, :], in_=score[:])

@@ -21,9 +21,10 @@ PASS = 512
 PICK = 512
 PAIR = 2 * P
 VECTOR_TILES = 36
-SCALAR_TILES = 4
+SCALAR_TILES = 8
+WARM_PASSES = 5
+HALF = S // 2
 V2_PLANE_ROW = (4, 8)
-WARM_PASSES = {(1, 1): 2, (1, 3): 3}
 
 
 def tile_list_duplicate_collision_score_kernel(
@@ -40,26 +41,25 @@ def tile_list_duplicate_collision_score_kernel(
         idx = lists.tile([P, S // 16], U16, name="idx")
         idx2 = lists.tile([P, S2 // 16], U16, name="idx2")
 
-        v2_planes = keep.tile([P, T2 // 4], I32, name="v2_planes", align_bytes=64)
+        v2_rows = keep.tile([P, T2 // 4], I32, name="v2_rows", align_bytes=64)
+        v2_scales = keep.tile([P, S2 // 4], I32, name="v2_scales", align_bytes=64)
         w4_planes = keep.tile([P, 2, H // 4], I32, name="w4_planes", align_bytes=64)
         v_planes = keep.tile([P, 2, T // 4], I32, name="v_planes", align_bytes=64)
         w4_raw = keep.tile([P, 2, H // 2], I32, name="w4_raw", align_bytes=64)
         gains = keep.tile([P, 2, 4], F32, name="gains")
         zero_in = keep.tile([P, 1], F32, name="zero_in")
         zero = keep.tile([P, 1], F32, name="zero")
-        w1_pass0 = keep.tile([P, 4, H], F32, name="w1_full0")
-        w1_raw = {(0, a): w1_pass0[:, :, a * PASS : (a + 1) * PASS] for a in range(2)}
-        for a in range(2):
-            w1_raw[1, a] = keep.tile([P, 4, PASS], F32, name="w1_pass1_%d" % a)
+        w1_rows = [keep.tile([P, 4, H], F32, name="w1_rows%d" % g) for g in range(2)]
         v_table = [keep.tile([P, T], I32, name="v_table%d" % g, align_bytes=64) for g in range(2)]
         v2_table = [keep.tile([P, T2], I32, name="v2_table%d" % a, align_bytes=64) for a in range(2)]
         w1_scales = keep.tile([P, 2 * H], U8, name="w1_scales", align_bytes=64)
         h_codes = keep.tile([P, 2, S], U32, name="h_codes", align_bytes=64)
         h_scales = keep.tile([P, 2, S], U8, name="h_scales", align_bytes=64)
 
-        nc.vector.memset(w4_planes[:], 0)
-        nc.vector.memset(v2_planes[:], 0)
+        nc.gpsimd.memset(v2_rows[:], 0)
         nc.vector.memset(v_planes[:], 0)
+        nc.vector.memset(w4_planes[:], 0)
+        nc.vector.memset(v2_scales[:], 0)
         nc.gpsimd.memset(zero_in[:], 0.0)
         nc.scalar.activation(zero[:], zero_in[:], ACT.Tanh)
 
@@ -73,24 +73,17 @@ def tile_list_duplicate_collision_score_kernel(
             for r in range(4):
                 nc.sync.dma_start(out=dst[r:P:32, :, :], in_=scales[:, r:16:4, :].rearrange("g q n -> q g n").bitcast(I32))
 
+        nc.sync.dma_start(idx[:], offs)
         nc.sync.dma_start(idx2[:], offs2)
         nc.sync.dma_start(out=w4_raw[:], in_=w4_words.rearrange("g p n -> p g n").bitcast(I32))
-        load_planes(w4_planes, w4_scales)
-        for r in range(4):
-            for a in range(2):
-                nc.sync.dma_start(
-                    out=v2_planes[V2_PLANE_ROW[a] + r : P : 32, :], in_=tab2_scales[a, r:16:4, :].bitcast(I32)
-                )
-        load_rows(w1_pass0, w1[:PASS, :])
-        nc.sync.dma_start(idx[:], offs)
+        nc.sync.dma_start(out=v2_rows[0:P:4, :], in_=tab2_scales.rearrange("a q n -> (a q) n").bitcast(I32))
         load_planes(v_planes, tab_scales)
+        load_rows(w1_rows[0], w1[:PASS, :])
         load_words(v_table[0], tab_words[0])
+        load_planes(w4_planes, w4_scales)
+        load_rows(w1_rows[1], w1[PASS:, :])
         nc.sync.dma_start(out=gains[:], in_=gain.rearrange("(a p t) -> p a t", a=2, t=4))
         load_words(v_table[1], tab_words[1])
-        for a in range(2):
-            load_rows(w1_raw[1, a], w1[PASS:, a * PASS : (a + 1) * PASS])
-        for a in range(2):
-            load_words(v2_table[a], tab2_words[a])
 
         def vector_tile(width, dtype):
             return ordered.tile([P, width], dtype, name="vector_out", align_bytes=64, bufs=VECTOR_TILES)
@@ -98,10 +91,9 @@ def tile_list_duplicate_collision_score_kernel(
         def scalar_tile(shape, dtype):
             return ordered.tile(shape, dtype, name="scalar_out", align_bytes=64, bufs=SCALAR_TILES)
 
-        def gather(window, offsets, q, dtype):
-            picked = vector_tile(PICK, dtype)
-            columns = PICK // 16
-            nc.vector.tensor_copy(picked[:], window.bitcast(dtype).indirect(offsets[:, columns * q : columns * (q + 1)]))
+        def gather(window, offsets, first, count, dtype):
+            picked = vector_tile(count, dtype)
+            nc.vector.tensor_copy(picked[:], window.bitcast(dtype).indirect(offsets[:, first // 16 : (first + count) // 16]))
             return picked
 
         def reorder_columns(raw, dtype):
@@ -112,14 +104,14 @@ def tile_list_duplicate_collision_score_kernel(
             )
             return moved
 
-        rounded, w1_codes, tanh_p, c_bank, h_rounded, v2_codes = {}, {}, {}, {}, {}, {}
+        rounded, w1_codes, p_bank, tanh_p, c_bank, h_rounded, v2_codes = {}, {}, {}, {}, {}, {}, {}
 
         def round_w1(g, a, u, on_vector):
             rounded[g, a, u] = vector_tile(4 * PAIR, BF16) if on_vector else scalar_tile([P, 4 * PAIR], BF16)
             copy = nc.vector.tensor_copy if on_vector else nc.scalar.copy
             copy(
                 out=rounded[g, a, u][:].rearrange("p (e m j) -> p m j e", e=2, j=4),
-                in_=w1_raw[g, a][:].rearrange("p j (m t) -> p m j t", t=4)[:, :, :, 2 * u : 2 * u + 2],
+                in_=w1_rows[g][:, :, a * PASS : (a + 1) * PASS].rearrange("p j (m t) -> p m j t", t=4)[:, :, :, 2 * u : 2 * u + 2],
             )
 
         def quantise_w1(g, a, u):
@@ -129,45 +121,54 @@ def tile_list_duplicate_collision_score_kernel(
                 out=w1_codes[g, a, u][:].bitcast(FP8X4), scales=w1_scales[:, first : first + PAIR], in_=rounded[g, a, u][:]
             )
 
-        def soft_code(a, t):
-            bank = psum.tile([P, S], F32, name="bank_a")
-            for g in range(2):
+        def project(g, a, half):
+            for t in range(4):
+                if g == 0 and t % 2 == 0:
+                    p_bank[a, half, t // 2] = psum.tile([P, 2, HALF], F32, name="bank_a")
                 first = g * H + a * PASS + t * P
                 nc.tensor.matmul_mx(
-                    out=bank[:],
+                    out=p_bank[a, half, t // 2][:, t % 2, :],
                     lhsT=w1_codes[g, a, t // 2][:, (t % 2) * P : (t % 2 + 1) * P].bitcast(FP8X4),
                     lhsT_scale=w1_scales[:, first : first + P],
-                    rhs=v_codes[g][:].bitcast(FP8X4),
-                    rhs_scale=v_scales[g][:],
-                    start=(g == 0),
-                    stop=(g == 1),
+                    rhs=v_codes[g, half].bitcast(FP8X4),
+                    rhs_scale=v_scales[g][:, half * HALF : (half + 1) * HALF],
+                    start=(g == 0 and t % 2 == 0),
+                    stop=(g == 1 and t % 2 == 1),
                 )
-            if a not in tanh_p:
-                tanh_p[a] = scalar_tile([P, 4, S], F32)
-            nc.scalar.activation(tanh_p[a][:, t, :], bank[:], ACT.Tanh, bias=zero[:], scale=gains[:, a, t : t + 1])
 
-        def signed_weights(a, b):
-            records = slice(b * P, (b + 1) * P)
-            c_bank[a, b] = psum.tile([P, 4, P], F32, name="bank_b")
+        def soft_code(a, half):
+            tanh_p[a, half] = scalar_tile([P, 4, HALF], F32)
             for t in range(4):
-                for g in range(2):
-                    first = a * PASS + t * P
-                    nc.tensor.matmul_mx(
-                        out=c_bank[a, b][:, t, :],
-                        lhsT=w4_codes[g][:, 2 * first : 2 * (first + P)].bitcast(FP4X4),
-                        lhsT_scale=w4_moved_scales[:, g * H + first : g * H + first + P],
-                        rhs=v_codes[g][:, records].bitcast(FP8X4),
-                        rhs_scale=v_scales[g][:, records],
-                        start=(g == 0),
-                        stop=(g == 1),
-                    )
+                nc.scalar.activation(
+                    tanh_p[a, half][:, t, :],
+                    p_bank[a, half, t // 2][:, t % 2, :],
+                    ACT.Tanh,
+                    bias=zero[:],
+                    scale=gains[:, a, t : t + 1],
+                )
+
+        def signed_weights(g, a, b):
+            records = slice(b * P, (b + 1) * P)
+            if g == 0:
+                c_bank[a, b] = psum.tile([P, 4, P], F32, name="bank_b")
+            for t in range(4):
+                first = a * PASS + t * P
+                nc.tensor.matmul_mx(
+                    out=c_bank[a, b][:, t, :],
+                    lhsT=w4_codes[g][:, 2 * first : 2 * (first + P)].bitcast(FP4X4),
+                    lhsT_scale=w4_moved_scales[:, g * H + first : g * H + first + P],
+                    rhs=v_codes[g, b // 2][:, (b % 2) * P : (b % 2 + 1) * P].bitcast(FP8X4),
+                    rhs_scale=v_scales[g][:, records],
+                    start=(g == 0 and t == 0),
+                    stop=(g == 1 and t == 3),
+                )
 
         def weighted_code(a, b):
             h_rounded[a, b] = vector_tile(4 * P, BF16)
             nc.vector.tensor_tensor(
                 out=h_rounded[a, b][:].rearrange("p (n i t) -> p n t i", i=2, t=4),
                 in0=c_bank[a, b][:].rearrange("p t (n i) -> p n t i", i=2),
-                in1=tanh_p[a][:, :, b * P : (b + 1) * P].rearrange("p t (n i) -> p n t i", i=2),
+                in1=tanh_p[a, b // 2][:, :, (b % 2) * P : (b % 2 + 1) * P].rearrange("p t (n i) -> p n t i", i=2),
                 op=MULT,
             )
 
@@ -178,60 +179,71 @@ def tile_list_duplicate_collision_score_kernel(
             )
 
         def pick_v2_words(q, a):
-            v2_codes[q, a] = gather(v2_table[a][:], idx2, q, U32)
+            v2_codes[q, a] = gather(v2_table[a][:], idx2, q * PICK, PICK, U32)
+
+        def move_v2_scales(a):
+            for r in range(4):
+                nc.sync.dma_start(
+                    out=v2_scales[V2_PLANE_ROW[a] + r : P : 32, :],
+                    in_=v2_picked[64 * a + 4 * r : 64 * (a + 1) : 16, :].bitcast(I32),
+                )
 
         w4_codes = [reorder_columns(w4_raw[:, g, :], U16) for g in range(2)]
-        w4_moved_scales = reorder_columns(w4_planes[:].rearrange("p g w -> p (g w)"), U8)
-        v2_scales = [gather(v2_planes[:], idx2, q, U8) for q in range(S2 // PICK)]
+        v2_picked = gather(v2_rows[:], idx2, 0, S2, U8)
+        v_scales = [gather(v_planes[:, g, :], idx, 0, S, U8) for g in range(2)]
+        for a in range(2):
+            move_v2_scales(a)
+            load_words(v2_table[a], tab2_words[a])
         for a in range(2):
             for u in range(2):
                 round_w1(0, a, u, on_vector=False)
-        v_scales = [gather(v_planes[:, g, :], idx, 0, U8) for g in range(2)]
+        for u in range(2):
+            quantise_w1(0, 0, u)
+        w4_moved_scales = reorder_columns(w4_planes[:].rearrange("p g w -> p (g w)"), U8)
+        for u in range(2):
+            quantise_w1(0, 1, u)
+        first_pass = gather(v_table[0][:], idx, 0, S, U32)
+        v_codes = {(0, half): first_pass[:, half * HALF : (half + 1) * HALF] for half in range(2)}
+        for half in range(2):
+            project(0, 0, half)
+        for b in range(4):
+            signed_weights(0, 0, b)
 
-        v_codes = []
-        for g in range(2):
-            v_codes.append(gather(v_table[g][:], idx, 0, U32))
-            for u in range(2):
-                quantise_w1(0, g, u)
+        for u in range(2):
+            round_w1(1, 0, u, on_vector=True)
+            round_w1(1, 1, u, on_vector=False)
+        quantise_w1(1, 0, 0)
+        quantise_w1(1, 0, 1)
+        quantise_w1(1, 1, 0)
+        for half in range(2):
+            v_codes[1, half] = gather(v_table[1][:], idx, half * HALF, HALF, U32)[:]
+        quantise_w1(1, 1, 1)
 
-        for b in range(4):
-            signed_weights(0, b)
-        round_w1(1, 0, 1, on_vector=True)
-        round_w1(1, 0, 0, on_vector=False)
-        for u in (1, 0):
-            quantise_w1(1, 0, u)
-        for t in (2, 3, 0, 1):
-            soft_code(0, t)
-        for u in (1, 0):
-            round_w1(1, 1, u, on_vector=True)
-        for u in (1, 0):
-            quantise_w1(1, 1, u)
-        for b in range(4):
-            weighted_code(0, b)
-        for b in range(4):
-            quantise_h(0, b)
-
-        for t in (2, 3, 0, 1):
-            soft_code(1, t)
-        for b in range(4):
-            signed_weights(1, b)
-        pick_v2_words(0, 0)
-        for b in range(4):
-            weighted_code(1, b)
-        for b in range(4):
-            quantise_h(1, b)
+        for a in range(2):
+            for half in range(2):
+                for g in range(1 - a, 2):
+                    project(g, a, half)
+                soft_code(a, half)
+                for b in (2 * half, 2 * half + 1):
+                    for g in range(1 - a, 2):
+                        signed_weights(g, a, b)
+            for b in range(4):
+                weighted_code(a, b)
+            for b in range(4):
+                quantise_h(a, b)
+            pick_v2_words(0, a)
 
         for q in range(S2 // PICK):
             for a in range(2):
                 if (q, a) not in v2_codes:
                     pick_v2_words(q, a)
-            banks = [psum.tile([P, S], F32, name="bank_a" if n % 2 == 0 else "bank_b") for n in range(4)]
-            for n in range(4):
-                for repeat in range(WARM_PASSES.get((q, n), 0)):
+            banks = [psum.tile([P, S], F32, name="bank_a" if q % 2 == 0 else "bank_b") for n in range(4)]
+            if q == 1:
+                for repeat in range(WARM_PASSES):
                     nc.tensor.matmul_mx(
-                        out=banks[n][:],
+                        out=banks[3][:],
                         lhsT=v2_codes[0, 0][:, :P].bitcast(FP8X4),
-                        lhsT_scale=v2_scales[0][V2_PLANE_ROW[0] : P, :P],
+                        lhsT_scale=v2_scales[V2_PLANE_ROW[0] : P, :].bitcast(U8)[:, :P],
                         rhs=h_codes[:, 0, :].bitcast(FP8X4),
                         rhs_scale=h_scales[:, 0, :],
                         start=True,
@@ -243,7 +255,7 @@ def tile_list_duplicate_collision_score_kernel(
                     nc.tensor.matmul_mx(
                         out=banks[n][:],
                         lhsT=v2_codes[q, a][:, candidates].bitcast(FP8X4),
-                        lhsT_scale=v2_scales[q][V2_PLANE_ROW[a] : P, candidates],
+                        lhsT_scale=v2_scales[V2_PLANE_ROW[a] : P, :].bitcast(U8)[:, q * PICK + n * P : q * PICK + (n + 1) * P],
                         rhs=h_codes[:, a, :].bitcast(FP8X4),
                         rhs_scale=h_scales[:, a, :],
                         start=(a == 0),

@@ -44,7 +44,8 @@ def tile_list_duplicate_collision_score_kernel(
         v2_rows = keep.tile([P, T2 // 4], I32, name="v2_rows", align_bytes=64)
         v2_scales = keep.tile([P, S2 // 4], I32, name="v2_scales", align_bytes=64)
         w4_planes = keep.tile([P, 2, H // 4], I32, name="w4_planes", align_bytes=64)
-        v_planes = keep.tile([P, 2, T // 4], I32, name="v_planes", align_bytes=64)
+        v_rows = keep.tile([P, T // 4], I32, name="v_rows", align_bytes=64)
+        v_planes = keep.tile([P, 2, S // 4], I32, name="v_planes", align_bytes=64)
         w4_raw = keep.tile([P, 2, H // 2], I32, name="w4_raw", align_bytes=64)
         gains = keep.tile([P, 2, 4], F32, name="gains")
         zero_in = keep.tile([P, 1], F32, name="zero_in")
@@ -57,8 +58,9 @@ def tile_list_duplicate_collision_score_kernel(
         h_scales = keep.tile([P, 2, S], U8, name="h_scales", align_bytes=64)
 
         nc.gpsimd.memset(v2_rows[:], 0)
-        nc.vector.memset(v_planes[:], 0)
+        nc.vector.memset(v_rows[:], 0)
         nc.vector.memset(w4_planes[:], 0)
+        nc.vector.memset(v_planes[:], 0)
         nc.vector.memset(v2_scales[:], 0)
         nc.gpsimd.memset(zero_in[:], 0.0)
         nc.scalar.activation(zero[:], zero_in[:], ACT.Tanh)
@@ -73,17 +75,14 @@ def tile_list_duplicate_collision_score_kernel(
             for r in range(4):
                 nc.sync.dma_start(out=dst[r:P:32, :, :], in_=scales[:, r:16:4, :].rearrange("g q n -> q g n").bitcast(I32))
 
+        nc.sync.dma_start(out=w4_raw[:], in_=w4_words.rearrange("g p n -> p g n").bitcast(I32))
         nc.sync.dma_start(idx[:], offs)
         nc.sync.dma_start(idx2[:], offs2)
-        nc.sync.dma_start(out=w4_raw[:], in_=w4_words.rearrange("g p n -> p g n").bitcast(I32))
         nc.sync.dma_start(out=v2_rows[0:P:4, :], in_=tab2_scales.rearrange("a q n -> (a q) n").bitcast(I32))
-        load_planes(v_planes, tab_scales)
+        nc.sync.dma_start(out=v_rows[0:P:4, :], in_=tab_scales.rearrange("a q n -> (a q) n").bitcast(I32))
         load_rows(w1_rows[0], w1[:PASS, :])
-        load_words(v_table[0], tab_words[0])
         load_planes(w4_planes, w4_scales)
-        load_rows(w1_rows[1], w1[PASS:, :])
-        nc.sync.dma_start(out=gains[:], in_=gain.rearrange("(a p t) -> p a t", a=2, t=4))
-        load_words(v_table[1], tab_words[1])
+        load_words(v_table[0], tab_words[0])
 
         def vector_tile(width, dtype):
             return ordered.tile([P, width], dtype, name="vector_out", align_bytes=64, bufs=VECTOR_TILES)
@@ -138,14 +137,16 @@ def tile_list_duplicate_collision_score_kernel(
 
         def soft_code(a, half):
             tanh_p[a, half] = scalar_tile([P, 4, HALF], F32)
-            for t in range(4):
-                nc.scalar.activation(
-                    tanh_p[a, half][:, t, :],
-                    p_bank[a, half, t // 2][:, t % 2, :],
-                    ACT.Tanh,
-                    bias=zero[:],
-                    scale=gains[:, a, t : t + 1],
-                )
+            width = P if (a, half) == (0, 0) else HALF
+            for first in range(0, HALF, width):
+                for t in range(4):
+                    nc.scalar.activation(
+                        tanh_p[a, half][:, t, first : first + width],
+                        p_bank[a, half, t // 2][:, t % 2, first : first + width],
+                        ACT.Tanh,
+                        bias=zero[:],
+                        scale=gains[:, a, t : t + 1],
+                    )
 
         def signed_weights(g, a, b):
             records = slice(b * P, (b + 1) * P)
@@ -181,18 +182,23 @@ def tile_list_duplicate_collision_score_kernel(
         def pick_v2_words(q, a):
             v2_codes[q, a] = gather(v2_table[a][:], idx2, q * PICK, PICK, U32)
 
-        def move_v2_scales(a):
+        def move_scales(plane, first_row, picked, a):
             for r in range(4):
                 nc.sync.dma_start(
-                    out=v2_scales[V2_PLANE_ROW[a] + r : P : 32, :],
-                    in_=v2_picked[64 * a + 4 * r : 64 * (a + 1) : 16, :].bitcast(I32),
+                    out=plane[first_row + r : P : 32, :], in_=picked[64 * a + 4 * r : 64 * (a + 1) : 16, :].bitcast(I32)
                 )
 
         w4_codes = [reorder_columns(w4_raw[:, g, :], U16) for g in range(2)]
+        v_picked = gather(v_rows[:], idx, 0, S, U8)
         v2_picked = gather(v2_rows[:], idx2, 0, S2, U8)
-        v_scales = [gather(v_planes[:, g, :], idx, 0, S, U8) for g in range(2)]
+        v_scales = [v_planes[:, g, :].bitcast(U8) for g in range(2)]
+        move_scales(v_planes[:, 0, :], 0, v_picked, 0)
+        load_rows(w1_rows[1], w1[PASS:, :])
+        nc.sync.dma_start(out=gains[:], in_=gain.rearrange("(a p t) -> p a t", a=2, t=4))
+        move_scales(v_planes[:, 1, :], 0, v_picked, 1)
+        load_words(v_table[1], tab_words[1])
         for a in range(2):
-            move_v2_scales(a)
+            move_scales(v2_scales, V2_PLANE_ROW[a], v2_picked, a)
             load_words(v2_table[a], tab2_words[a])
         for a in range(2):
             for u in range(2):
@@ -224,7 +230,7 @@ def tile_list_duplicate_collision_score_kernel(
                 for g in range(1 - a, 2):
                     project(g, a, half)
                 soft_code(a, half)
-                for b in (2 * half, 2 * half + 1):
+                for b in ((0,), (1, 2, 3))[half]:
                     for g in range(1 - a, 2):
                         signed_weights(g, a, b)
             for b in range(4):

@@ -57,7 +57,7 @@ def tile_list_duplicate_collision_score_kernel(
         h_codes = keep.tile([P, 2, S], U32, name="h_codes", align_bytes=64)
         h_scales = keep.tile([P, 2, S], U8, name="h_scales", align_bytes=64)
 
-        nc.gpsimd.memset(v2_rows[:], 0)
+        nc.vector.memset(v2_rows[:], 0)
         nc.vector.memset(v_rows[:], 0)
         nc.vector.memset(w4_planes[:], 0)
         nc.vector.memset(v_planes[:], 0)
@@ -137,7 +137,7 @@ def tile_list_duplicate_collision_score_kernel(
 
         def soft_code(a, half):
             tanh_p[a, half] = scalar_tile([P, 4, HALF], F32)
-            width = P if (a, half) == (0, 0) else HALF
+            width = P if a == 0 else HALF
             for first in range(0, HALF, width):
                 for t in range(4):
                     nc.scalar.activation(
@@ -182,9 +182,9 @@ def tile_list_duplicate_collision_score_kernel(
         def pick_v2_words(q, a):
             v2_codes[q, a] = gather(v2_table[a][:], idx2, q * PICK, PICK, U32)
 
-        def move_scales(plane, first_row, picked, a):
+        def move_scales(queue, plane, first_row, picked, a):
             for r in range(4):
-                nc.sync.dma_start(
+                queue.dma_start(
                     out=plane[first_row + r : P : 32, :], in_=picked[64 * a + 4 * r : 64 * (a + 1) : 16, :].bitcast(I32)
                 )
 
@@ -192,13 +192,13 @@ def tile_list_duplicate_collision_score_kernel(
         v_picked = gather(v_rows[:], idx, 0, S, U8)
         v2_picked = gather(v2_rows[:], idx2, 0, S2, U8)
         v_scales = [v_planes[:, g, :].bitcast(U8) for g in range(2)]
-        move_scales(v_planes[:, 0, :], 0, v_picked, 0)
+        move_scales(nc.sync, v_planes[:, 0, :], 0, v_picked, 0)
         load_rows(w1_rows[1], w1[PASS:, :])
-        nc.sync.dma_start(out=gains[:], in_=gain.rearrange("(a p t) -> p a t", a=2, t=4))
-        move_scales(v_planes[:, 1, :], 0, v_picked, 1)
+        move_scales(nc.sync, v_planes[:, 1, :], 0, v_picked, 1)
         load_words(v_table[1], tab_words[1])
+        nc.sync.dma_start(out=gains[:], in_=gain.rearrange("(a p t) -> p a t", a=2, t=4))
         for a in range(2):
-            move_scales(v2_scales, V2_PLANE_ROW[a], v2_picked, a)
+            move_scales(nc.sync, v2_scales, V2_PLANE_ROW[a], v2_picked, a)
             load_words(v2_table[a], tab2_words[a])
         for a in range(2):
             for u in range(2):
@@ -206,9 +206,9 @@ def tile_list_duplicate_collision_score_kernel(
         for u in range(2):
             quantise_w1(0, 0, u)
         w4_moved_scales = reorder_columns(w4_planes[:].rearrange("p g w -> p (g w)"), U8)
+        first_pass = gather(v_table[0][:], idx, 0, S, U32)
         for u in range(2):
             quantise_w1(0, 1, u)
-        first_pass = gather(v_table[0][:], idx, 0, S, U32)
         v_codes = {(0, half): first_pass[:, half * HALF : (half + 1) * HALF] for half in range(2)}
         for half in range(2):
             project(0, 0, half)

@@ -73,7 +73,7 @@ def tile_list_duplicate_collision_score_kernel(
 
         def load_planes(dst, scales):
             for r in range(4):
-                nc.sync.dma_start(out=dst[r:P:32, :, :], in_=scales[:, r:16:4, :].rearrange("g q n -> q g n").bitcast(I32))
+                nc.gpsimd.dma_start(out=dst[r:P:32, :, :], in_=scales[:, r:16:4, :].rearrange("g q n -> q g n").bitcast(I32))
 
         nc.sync.dma_start(out=w4_raw[:], in_=w4_words.rearrange("g p n -> p g n").bitcast(I32))
         nc.sync.dma_start(idx[:], offs)
@@ -198,7 +198,7 @@ def tile_list_duplicate_collision_score_kernel(
         load_words(v_table[1], tab_words[1])
         nc.sync.dma_start(out=gains[:], in_=gain.rearrange("(a p t) -> p a t", a=2, t=4))
         for a in range(2):
-            move_scales(nc.sync, v2_scales, V2_PLANE_ROW[a], v2_picked, a)
+            move_scales(nc.gpsimd, v2_scales, V2_PLANE_ROW[a], v2_picked, a)
             load_words(v2_table[a], tab2_words[a])
         for a in range(2):
             for u in range(2):

@@ -22,7 +22,7 @@ PICK = 512
 PAIR = 2 * P
 VECTOR_TILES = 36
 SCALAR_TILES = 8
-WARM_PASSES = 5
+WARM_PASSES = 6
 HALF = S // 2
 V2_PLANE_ROW = (4, 8)
 
@@ -36,7 +36,7 @@ def tile_list_duplicate_collision_score_kernel(
         keep = ctx.enter_context(tc.tile_pool(name="keep", bufs=1))
         ordered = ctx.enter_context(tc.tile_pool(name="ordered", bufs=1))
         stage = ctx.enter_context(tc.tile_pool(name="stage", bufs=S2 // P))
-        psum = ctx.enter_context(tc.psum_pool(name="psum", bufs=4))
+        psum = ctx.enter_context(tc.psum_pool(name="psum", bufs=1))
 
         idx = lists.tile([P, S // 16], U16, name="idx")
         idx2 = lists.tile([P, S2 // 16], U16, name="idx2")
@@ -54,7 +54,6 @@ def tile_list_duplicate_collision_score_kernel(
         v_table = [keep.tile([P, T], I32, name="v_table%d" % g, align_bytes=64) for g in range(2)]
         v2_table = [keep.tile([P, T2], I32, name="v2_table%d" % a, align_bytes=64) for a in range(2)]
         w1_scales = keep.tile([P, 2 * H], U8, name="w1_scales", align_bytes=64)
-        h_codes = keep.tile([P, 2, S], U32, name="h_codes", align_bytes=64)
         h_scales = keep.tile([P, 2, S], U8, name="h_scales", align_bytes=64)
 
         nc.vector.memset(v2_rows[:], 0)
@@ -103,7 +102,7 @@ def tile_list_duplicate_collision_score_kernel(
             )
             return moved
 
-        rounded, w1_codes, p_bank, tanh_p, c_bank, h_rounded, v2_codes = {}, {}, {}, {}, {}, {}, {}
+        rounded, w1_codes, p_bank, tanh_p, c_bank, h_rounded, h_codes, v2_codes = {}, {}, {}, {}, {}, {}, {}, {}
 
         def round_w1(g, a, u, on_vector):
             rounded[g, a, u] = vector_tile(4 * PAIR, BF16) if on_vector else scalar_tile([P, 4 * PAIR], BF16)
@@ -123,7 +122,7 @@ def tile_list_duplicate_collision_score_kernel(
         def project(g, a, half):
             for t in range(4):
                 if g == 0 and t % 2 == 0:
-                    p_bank[a, half, t // 2] = psum.tile([P, 2, HALF], F32, name="bank_a")
+                    p_bank[a, half, t // 2] = psum.tile([P, 2, HALF], F32, name="bank%d" % (2 * half + t // 2))
                 first = g * H + a * PASS + t * P
                 nc.tensor.matmul_mx(
                     out=p_bank[a, half, t // 2][:, t % 2, :],
@@ -137,12 +136,11 @@ def tile_list_duplicate_collision_score_kernel(
 
         def soft_code(a, half):
             tanh_p[a, half] = scalar_tile([P, 4, HALF], F32)
-            width = P if a == 0 else HALF
-            for first in range(0, HALF, width):
+            for first in range(0, HALF, P):
                 for t in range(4):
                     nc.scalar.activation(
-                        tanh_p[a, half][:, t, first : first + width],
-                        p_bank[a, half, t // 2][:, t % 2, first : first + width],
+                        tanh_p[a, half][:, t, first : first + P],
+                        p_bank[a, half, t // 2][:, t % 2, first : first + P],
                         ACT.Tanh,
                         bias=zero[:],
                         scale=gains[:, a, t : t + 1],
@@ -151,7 +149,7 @@ def tile_list_duplicate_collision_score_kernel(
         def signed_weights(g, a, b):
             records = slice(b * P, (b + 1) * P)
             if g == 0:
-                c_bank[a, b] = psum.tile([P, 4, P], F32, name="bank_b")
+                c_bank[a, b] = psum.tile([P, 4, P], F32, name="bank%d" % (4 + b))
             for t in range(4):
                 first = a * PASS + t * P
                 nc.tensor.matmul_mx(
@@ -165,18 +163,20 @@ def tile_list_duplicate_collision_score_kernel(
                 )
 
         def weighted_code(a, b):
-            h_rounded[a, b] = vector_tile(4 * P, BF16)
+            if b % 2 == 0:
+                h_rounded[a, b // 2] = vector_tile(4 * HALF, BF16)
             nc.vector.tensor_tensor(
-                out=h_rounded[a, b][:].rearrange("p (n i t) -> p n t i", i=2, t=4),
+                out=h_rounded[a, b // 2][:, (b % 2) * 4 * P : (b % 2 + 1) * 4 * P].rearrange("p (n i t) -> p n t i", i=2, t=4),
                 in0=c_bank[a, b][:].rearrange("p t (n i) -> p n t i", i=2),
                 in1=tanh_p[a, b // 2][:, :, (b % 2) * P : (b % 2 + 1) * P].rearrange("p t (n i) -> p n t i", i=2),
                 op=MULT,
             )
 
-        def quantise_h(a, b):
-            records = slice(b * P, (b + 1) * P)
+        def quantise_h(a, half):
+            records = slice(half * HALF, (half + 1) * HALF)
+            h_codes[a, half] = vector_tile(HALF, U32)
             nc.vector.quantize_mx(
-                out=h_codes[:, a, records].bitcast(FP8X4), scales=h_scales[:, a, records], in_=h_rounded[a, b][:]
+                out=h_codes[a, half][:].bitcast(FP8X4), scales=h_scales[:, a, records], in_=h_rounded[a, half][:]
             )
 
         def pick_v2_words(q, a):
@@ -220,9 +220,9 @@ def tile_list_duplicate_collision_score_kernel(
             round_w1(1, 1, u, on_vector=False)
         quantise_w1(1, 0, 0)
         quantise_w1(1, 0, 1)
-        quantise_w1(1, 1, 0)
         for half in range(2):
             v_codes[1, half] = gather(v_table[1][:], idx, half * HALF, HALF, U32)[:]
+        quantise_w1(1, 1, 0)
         quantise_w1(1, 1, 1)
 
         for a in range(2):
@@ -230,44 +230,50 @@ def tile_list_duplicate_collision_score_kernel(
                 for g in range(1 - a, 2):
                     project(g, a, half)
                 soft_code(a, half)
-                for b in ((0,), (1, 2, 3))[half]:
+                for b in (((0,), (1, 2, 3)), ((0, 1), (2, 3)))[a][half]:
                     for g in range(1 - a, 2):
                         signed_weights(g, a, b)
-            for b in range(4):
-                weighted_code(a, b)
-            for b in range(4):
-                quantise_h(a, b)
-            pick_v2_words(0, a)
+        for b in range(3):
+            weighted_code(0, b)
+        quantise_h(0, 0)
+        weighted_code(0, 3)
+        pick_v2_words(0, 0)
+        quantise_h(0, 1)
+        for b in range(3):
+            weighted_code(1, b)
+        quantise_h(1, 0)
+        weighted_code(1, 3)
+        pick_v2_words(0, 1)
+        quantise_h(1, 1)
 
+        def score_pass(bank, q, a, n, half, start, stop):
+            records = slice(half * HALF, (half + 1) * HALF)
+            nc.tensor.matmul_mx(
+                out=bank[:, records],
+                lhsT=v2_codes[q, a][:, n * P : (n + 1) * P].bitcast(FP8X4),
+                lhsT_scale=v2_scales[V2_PLANE_ROW[a] : P, :].bitcast(U8)[:, q * PICK + n * P : q * PICK + (n + 1) * P],
+                rhs=h_codes[a, half][:].bitcast(FP8X4),
+                rhs_scale=h_scales[:, a, records],
+                start=start,
+                stop=stop,
+            )
+
+        score_banks = [psum.tile([P, S], F32, name="bank%d" % (n % 8)) for n in range(S2 // P)]
         for q in range(S2 // PICK):
             for a in range(2):
                 if (q, a) not in v2_codes:
                     pick_v2_words(q, a)
-            banks = [psum.tile([P, S], F32, name="bank_a" if q % 2 == 0 else "bank_b") for n in range(4)]
-            if q == 1:
-                for repeat in range(WARM_PASSES):
-                    nc.tensor.matmul_mx(
-                        out=banks[3][:],
-                        lhsT=v2_codes[0, 0][:, :P].bitcast(FP8X4),
-                        lhsT_scale=v2_scales[V2_PLANE_ROW[0] : P, :].bitcast(U8)[:, :P],
-                        rhs=h_codes[:, 0, :].bitcast(FP8X4),
-                        rhs_scale=h_scales[:, 0, :],
-                        start=True,
-                        stop=True,
-                    )
+            banks = score_banks[4 * q : 4 * q + 4]
             for a in range(2):
+                if q == 0 and a == 1:
+                    for repeat in range(WARM_PASSES):
+                        score_pass(score_banks[7], 0, 0, 0, 0, True, True)
                 for n in range(4):
-                    candidates = slice(n * P, (n + 1) * P)
-                    nc.tensor.matmul_mx(
-                        out=banks[n][:],
-                        lhsT=v2_codes[q, a][:, candidates].bitcast(FP8X4),
-                        lhsT_scale=v2_scales[V2_PLANE_ROW[a] : P, :].bitcast(U8)[:, q * PICK + n * P : q * PICK + (n + 1) * P],
-                        rhs=h_codes[:, a, :].bitcast(FP8X4),
-                        rhs_scale=h_scales[:, a, :],
-                        start=(a == 0),
-                        stop=(a == 1),
-                    )
+                    for half in range(2):
+                        score_pass(banks[n], q, a, n, half, a == 0 and half == 0, a == 1 and half == 1)
                     if a == 1:
                         score = stage.tile([P, S], F32, name="score")
-                        nc.scalar.activation(score[:], banks[n][:], ACT.Abs)
-                        nc.sync.dma_start(out=out[q * PICK + n * P : q * PICK + (n + 1) * P, :], in_=score[:])
+                        rows = slice(q * PICK + n * P, q * PICK + (n + 1) * P)
+                        for records in (slice(0, HALF), slice(HALF, S)) if q + n == 0 else (slice(0, S),):
+                            nc.scalar.activation(score[:, records], banks[n][:, records], ACT.Abs)
+                            nc.sync.dma_start(out=out[rows, records], in_=score[:, records])

@@ -21,8 +21,9 @@ PASS = 512
 PICK = 512
 PAIR = 2 * P
 VECTOR_TILES = 36
-SCALAR_TILES = 8
-WARM_PASSES = 6
+SCALAR_TILES = 9
+WARM_PASSES = 8
+EARLY = S + PICK + H
 HALF = S // 2
 V2_PLANE_ROW = (4, 8)
 
@@ -42,15 +43,19 @@ def tile_list_duplicate_collision_score_kernel(
         idx2 = lists.tile([P, S2 // 16], U16, name="idx2")
 
         v2_rows = keep.tile([P, T2 // 4], I32, name="v2_rows", align_bytes=64)
-        v2_scales = keep.tile([P, S2 // 4], I32, name="v2_scales", align_bytes=64)
-        w4_planes = keep.tile([P, 2, H // 4], I32, name="w4_planes", align_bytes=64)
+        late_planes = keep.tile([P, (S2 - PICK) // 4], I32, name="late_planes", align_bytes=64)
+        w4_rows = keep.tile([P, H // 4], I32, name="w4_rows", align_bytes=64)
+        early_rows = keep.tile([P, EARLY], U8, name="early_rows", align_bytes=64)
         v_rows = keep.tile([P, T // 4], I32, name="v_rows", align_bytes=64)
-        v_planes = keep.tile([P, 2, S // 4], I32, name="v_planes", align_bytes=64)
+        early_planes = keep.tile([P, 2, EARLY // 4], I32, name="early_planes", align_bytes=64)
         w4_raw = keep.tile([P, 2, H // 2], I32, name="w4_raw", align_bytes=64)
         gains = keep.tile([P, 2, 4], F32, name="gains")
         zero_in = keep.tile([P, 1], F32, name="zero_in")
         zero = keep.tile([P, 1], F32, name="zero")
-        w1_rows = [keep.tile([P, 4, H], F32, name="w1_rows%d" % g) for g in range(2)]
+        w1_first = keep.tile([P, 4, H], F32, name="w1_first")
+        w1_second = [keep.tile([P, 4, PASS], F32, name="w1_second%d" % a) for a in range(2)]
+        w1_rows = {(0, a): w1_first[:, :, a * PASS : (a + 1) * PASS] for a in range(2)}
+        w1_rows.update({(1, a): w1_second[a][:] for a in range(2)})
         v_table = [keep.tile([P, T], I32, name="v_table%d" % g, align_bytes=64) for g in range(2)]
         v2_table = [keep.tile([P, T2], I32, name="v2_table%d" % a, align_bytes=64) for a in range(2)]
         w1_scales = keep.tile([P, 2 * H], U8, name="w1_scales", align_bytes=64)
@@ -58,9 +63,9 @@ def tile_list_duplicate_collision_score_kernel(
 
         nc.vector.memset(v2_rows[:], 0)
         nc.vector.memset(v_rows[:], 0)
-        nc.vector.memset(w4_planes[:], 0)
-        nc.vector.memset(v_planes[:], 0)
-        nc.vector.memset(v2_scales[:], 0)
+        nc.vector.memset(w4_rows[:], 0)
+        nc.vector.memset(early_planes[:], 0)
+        nc.vector.memset(late_planes[:], 0)
         nc.gpsimd.memset(zero_in[:], 0.0)
         nc.scalar.activation(zero[:], zero_in[:], ACT.Tanh)
 
@@ -70,17 +75,13 @@ def tile_list_duplicate_collision_score_kernel(
         def load_words(dst, words):
             nc.sync.dma_start(out=dst[:], in_=words.rearrange("p t i -> p (t i)").bitcast(I32))
 
-        def load_planes(dst, scales):
-            for r in range(4):
-                nc.gpsimd.dma_start(out=dst[r:P:32, :, :], in_=scales[:, r:16:4, :].rearrange("g q n -> q g n").bitcast(I32))
-
         nc.sync.dma_start(out=w4_raw[:], in_=w4_words.rearrange("g p n -> p g n").bitcast(I32))
         nc.sync.dma_start(idx[:], offs)
         nc.sync.dma_start(idx2[:], offs2)
         nc.sync.dma_start(out=v2_rows[0:P:4, :], in_=tab2_scales.rearrange("a q n -> (a q) n").bitcast(I32))
         nc.sync.dma_start(out=v_rows[0:P:4, :], in_=tab_scales.rearrange("a q n -> (a q) n").bitcast(I32))
-        load_rows(w1_rows[0], w1[:PASS, :])
-        load_planes(w4_planes, w4_scales)
+        nc.sync.dma_start(out=w4_rows[0:P:4, :], in_=w4_scales.rearrange("a q n -> (a q) n").bitcast(I32))
+        load_rows(w1_first, w1[:PASS, :])
         load_words(v_table[0], tab_words[0])
 
         def vector_tile(width, dtype):
@@ -89,15 +90,14 @@ def tile_list_duplicate_collision_score_kernel(
         def scalar_tile(shape, dtype):
             return ordered.tile(shape, dtype, name="scalar_out", align_bytes=64, bufs=SCALAR_TILES)
 
-        def gather(window, offsets, first, count, dtype):
-            picked = vector_tile(count, dtype)
-            nc.vector.tensor_copy(picked[:], window.bitcast(dtype).indirect(offsets[:, first // 16 : (first + count) // 16]))
+        def gather(window, offsets, first, count, dtype, picked=None):
+            picked = vector_tile(count, dtype)[:] if picked is None else picked
+            nc.vector.tensor_copy(picked, window.bitcast(dtype).indirect(offsets[:, first // 16 : (first + count) // 16]))
             return picked
 
-        def reorder_columns(raw, dtype):
-            moved = vector_tile(2 * H, U8)
+        def reorder_columns(raw, dtype, moved):
             nc.vector.tensor_copy(
-                out=moved[:].bitcast(dtype).rearrange("p (b t m) -> p b t m", t=4, m=P),
+                out=moved.bitcast(dtype).rearrange("p (b t m) -> p b t m", t=4, m=P),
                 in_=raw.bitcast(dtype).rearrange("p (b m t) -> p b t m", t=4, m=P),
             )
             return moved
@@ -109,7 +109,7 @@ def tile_list_duplicate_collision_score_kernel(
             copy = nc.vector.tensor_copy if on_vector else nc.scalar.copy
             copy(
                 out=rounded[g, a, u][:].rearrange("p (e m j) -> p m j e", e=2, j=4),
-                in_=w1_rows[g][:, :, a * PASS : (a + 1) * PASS].rearrange("p j (m t) -> p m j t", t=4)[:, :, :, 2 * u : 2 * u + 2],
+                in_=w1_rows[g, a].rearrange("p j (m t) -> p m j t", t=4)[:, :, :, 2 * u : 2 * u + 2],
             )
 
         def quantise_w1(g, a, u):
@@ -155,7 +155,7 @@ def tile_list_duplicate_collision_score_kernel(
                 nc.tensor.matmul_mx(
                     out=c_bank[a, b][:, t, :],
                     lhsT=w4_codes[g][:, 2 * first : 2 * (first + P)].bitcast(FP4X4),
-                    lhsT_scale=w4_moved_scales[:, g * H + first : g * H + first + P],
+                    lhsT_scale=w4_moved_scales[g][:, first : first + P],
                     rhs=v_codes[g, b // 2][:, (b % 2) * P : (b % 2 + 1) * P].bitcast(FP8X4),
                     rhs_scale=v_scales[g][:, records],
                     start=(g == 0 and t == 0),
@@ -182,78 +182,105 @@ def tile_list_duplicate_collision_score_kernel(
         def pick_v2_words(q, a):
             v2_codes[q, a] = gather(v2_table[a][:], idx2, q * PICK, PICK, U32)
 
-        def move_scales(queue, plane, first_row, picked, a):
+        def move_scales(plane, first_row, picked, a):
             for r in range(4):
-                queue.dma_start(
+                nc.sync.dma_start(
                     out=plane[first_row + r : P : 32, :], in_=picked[64 * a + 4 * r : 64 * (a + 1) : 16, :].bitcast(I32)
                 )
 
-        w4_codes = [reorder_columns(w4_raw[:, g, :], U16) for g in range(2)]
-        v_picked = gather(v_rows[:], idx, 0, S, U8)
-        v2_picked = gather(v2_rows[:], idx2, 0, S2, U8)
-        v_scales = [v_planes[:, g, :].bitcast(U8) for g in range(2)]
-        move_scales(nc.sync, v_planes[:, 0, :], 0, v_picked, 0)
-        load_rows(w1_rows[1], w1[PASS:, :])
-        move_scales(nc.sync, v_planes[:, 1, :], 0, v_picked, 1)
-        load_words(v_table[1], tab_words[1])
+        w4_codes = [reorder_columns(w4_raw[:, 0, :], U16, vector_tile(2 * H, U8)[:])]
+        early_picked = vector_tile(S + PICK, U8)
+        gather(v_rows[:], idx, 0, S, U8, early_picked[:, :S])
+        gather(v2_rows[:], idx2, 0, PICK, U8, early_picked[:, S:])
+        reorder_columns(w4_rows[:], U8, early_rows[:, S + PICK :])
+        nc.vector.tensor_copy(early_rows[:, : S + PICK].bitcast(I32), early_picked[:].bitcast(I32))
+        w4_codes.append(reorder_columns(w4_raw[:, 1, :], U16, vector_tile(2 * H, U8)[:]))
+        v_scales = [early_planes[:, g, :].bitcast(U8)[:, :S] for g in range(2)]
+        v2_scales = {(0, a): early_planes[:, a, :].bitcast(U8)[:, S : S + PICK] for a in range(2)}
+        w4_moved_scales = [early_planes[:, g, :].bitcast(U8)[:, S + PICK :] for g in range(2)]
+        for q in range(1, S2 // PICK):
+            for a in range(2):
+                v2_scales[q, a] = late_planes[V2_PLANE_ROW[a] :, :].bitcast(U8)[:, (q - 1) * PICK : q * PICK]
+        move_scales(early_planes[:, 0, :], 0, early_rows, 0)
+        load_rows(w1_second[0], w1[PASS:, :PASS])
         nc.sync.dma_start(out=gains[:], in_=gain.rearrange("(a p t) -> p a t", a=2, t=4))
+        move_scales(early_planes[:, 1, :], 0, early_rows, 1)
+        load_words(v_table[1], tab_words[1])
+        load_rows(w1_second[1], w1[PASS:, PASS:])
         for a in range(2):
-            move_scales(nc.gpsimd, v2_scales, V2_PLANE_ROW[a], v2_picked, a)
             load_words(v2_table[a], tab2_words[a])
+
         for a in range(2):
             for u in range(2):
                 round_w1(0, a, u, on_vector=False)
-        for u in range(2):
-            quantise_w1(0, 0, u)
-        w4_moved_scales = reorder_columns(w4_planes[:].rearrange("p g w -> p (g w)"), U8)
+        quantise_w1(0, 0, 0)
         first_pass = gather(v_table[0][:], idx, 0, S, U32)
-        for u in range(2):
-            quantise_w1(0, 1, u)
+        quantise_w1(0, 0, 1)
+        late_picked = gather(v2_rows[:], idx2, PICK, S2 - PICK, U8)
+        for a in range(2):
+            move_scales(late_planes, V2_PLANE_ROW[a], late_picked, a)
         v_codes = {(0, half): first_pass[:, half * HALF : (half + 1) * HALF] for half in range(2)}
         for half in range(2):
             project(0, 0, half)
         for b in range(4):
             signed_weights(0, 0, b)
 
-        for u in range(2):
-            round_w1(1, 0, u, on_vector=True)
-            round_w1(1, 1, u, on_vector=False)
+        round_w1(1, 0, 0, on_vector=True)
+        round_w1(1, 0, 1, on_vector=False)
+        quantise_w1(0, 1, 0)
         quantise_w1(1, 0, 0)
         quantise_w1(1, 0, 1)
+        quantise_w1(0, 1, 1)
         for half in range(2):
-            v_codes[1, half] = gather(v_table[1][:], idx, half * HALF, HALF, U32)[:]
+            v_codes[1, half] = gather(v_table[1][:], idx, half * HALF, HALF, U32)
+
+        project(1, 0, 0)
+        soft_code(0, 0)
+        signed_weights(1, 0, 0)
+        signed_weights(1, 0, 1)
+        project(1, 0, 1)
+        signed_weights(1, 0, 2)
+        signed_weights(1, 0, 3)
+        round_w1(1, 1, 1, on_vector=False)
+        round_w1(1, 1, 0, on_vector=True)
+        soft_code(0, 1)
+        weighted_code(0, 0)
+        weighted_code(0, 1)
         quantise_w1(1, 1, 0)
         quantise_w1(1, 1, 1)
-
-        for a in range(2):
-            for half in range(2):
-                for g in range(1 - a, 2):
-                    project(g, a, half)
-                soft_code(a, half)
-                for b in (((0,), (1, 2, 3)), ((0, 1), (2, 3)))[a][half]:
-                    for g in range(1 - a, 2):
-                        signed_weights(g, a, b)
-        for b in range(3):
-            weighted_code(0, b)
         quantise_h(0, 0)
+        project(0, 1, 0)
+        for b in range(2):
+            for g in range(2):
+                signed_weights(g, 1, b)
+        project(1, 1, 0)
+        soft_code(1, 0)
+        weighted_code(0, 2)
         weighted_code(0, 3)
-        pick_v2_words(0, 0)
+        for g in range(2):
+            project(g, 1, 1)
+        soft_code(1, 1)
+        for b in range(2, 4):
+            for g in range(2):
+                signed_weights(g, 1, b)
         quantise_h(0, 1)
-        for b in range(3):
-            weighted_code(1, b)
-        quantise_h(1, 0)
+        weighted_code(1, 0)
+        weighted_code(1, 1)
+        pick_v2_words(0, 0)
+        weighted_code(1, 2)
         weighted_code(1, 3)
+        for half in range(2):
+            quantise_h(1, half)
         pick_v2_words(0, 1)
-        quantise_h(1, 1)
 
-        def score_pass(bank, q, a, n, half, start, stop):
+        def score_pass(bank, q, a, n, half, start, stop, codes_of=None):
             records = slice(half * HALF, (half + 1) * HALF)
             nc.tensor.matmul_mx(
                 out=bank[:, records],
                 lhsT=v2_codes[q, a][:, n * P : (n + 1) * P].bitcast(FP8X4),
-                lhsT_scale=v2_scales[V2_PLANE_ROW[a] : P, :].bitcast(U8)[:, q * PICK + n * P : q * PICK + (n + 1) * P],
-                rhs=h_codes[a, half][:].bitcast(FP8X4),
-                rhs_scale=h_scales[:, a, records],
+                lhsT_scale=v2_scales[q, a][:, n * P : (n + 1) * P],
+                rhs=h_codes[a if codes_of is None else codes_of, half][:].bitcast(FP8X4),
+                rhs_scale=h_scales[:, a if codes_of is None else codes_of, records],
                 start=start,
                 stop=stop,
             )
@@ -267,7 +294,7 @@ def tile_list_duplicate_collision_score_kernel(
             for a in range(2):
                 if q == 0 and a == 1:
                     for repeat in range(WARM_PASSES):
-                        score_pass(score_banks[7], 0, 0, 0, 0, True, True)
+                        score_pass(score_banks[7], 0, 0, 0, 1, True, True, codes_of=1)
                 for n in range(4):
                     for half in range(2):
                         score_pass(banks[n], q, a, n, half, a == 0 and half == 0, a == 1 and half == 1)

@@ -15,13 +15,14 @@ FP8X4 = mybir.dt.float8_e4m3fn_x4
 FP4X4 = mybir.dt.float4_e2m1fn_x4
 ACT = mybir.ActivationFunctionType
 MULT = mybir.AluOpType.mult
+MAX = mybir.AluOpType.max
 
 P = 128
 PASS = 512
 PICK = 512
 PAIR = 2 * P
 VECTOR_TILES = 36
-SCALAR_TILES = 9
+SCALAR_TILES = 8
 WARM_PASSES = 8
 EARLY = S + PICK + H
 HALF = S // 2
@@ -48,7 +49,7 @@ def tile_list_duplicate_collision_score_kernel(
         early_rows = keep.tile([P, EARLY], U8, name="early_rows", align_bytes=64)
         v_rows = keep.tile([P, T // 4], I32, name="v_rows", align_bytes=64)
         early_planes = keep.tile([P, 2, EARLY // 4], I32, name="early_planes", align_bytes=64)
-        w4_raw = keep.tile([P, 2, H // 2], I32, name="w4_raw", align_bytes=64)
+        w4_raw = [keep.tile([P, H // 2], I32, name="w4_raw%d" % g, align_bytes=64) for g in range(2)]
         gains = keep.tile([P, 2, 4], F32, name="gains")
         zero_in = keep.tile([P, 1], F32, name="zero_in")
         zero = keep.tile([P, 1], F32, name="zero")
@@ -61,9 +62,9 @@ def tile_list_duplicate_collision_score_kernel(
         w1_scales = keep.tile([P, 2 * H], U8, name="w1_scales", align_bytes=64)
         h_scales = keep.tile([P, 2, S], U8, name="h_scales", align_bytes=64)
 
+        nc.vector.memset(w4_rows[:], 0)
         nc.vector.memset(v2_rows[:], 0)
         nc.vector.memset(v_rows[:], 0)
-        nc.vector.memset(w4_rows[:], 0)
         nc.vector.memset(early_planes[:], 0)
         nc.vector.memset(late_planes[:], 0)
         nc.gpsimd.memset(zero_in[:], 0.0)
@@ -75,12 +76,13 @@ def tile_list_duplicate_collision_score_kernel(
         def load_words(dst, words):
             nc.sync.dma_start(out=dst[:], in_=words.rearrange("p t i -> p (t i)").bitcast(I32))
 
-        nc.sync.dma_start(out=w4_raw[:], in_=w4_words.rearrange("g p n -> p g n").bitcast(I32))
+        for g in range(2):
+            nc.sync.dma_start(out=w4_raw[g][:], in_=w4_words[g].bitcast(I32))
         nc.sync.dma_start(idx[:], offs)
         nc.sync.dma_start(idx2[:], offs2)
+        nc.sync.dma_start(out=w4_rows[0:P:4, :], in_=w4_scales.rearrange("a q n -> (a q) n").bitcast(I32))
         nc.sync.dma_start(out=v2_rows[0:P:4, :], in_=tab2_scales.rearrange("a q n -> (a q) n").bitcast(I32))
         nc.sync.dma_start(out=v_rows[0:P:4, :], in_=tab_scales.rearrange("a q n -> (a q) n").bitcast(I32))
-        nc.sync.dma_start(out=w4_rows[0:P:4, :], in_=w4_scales.rearrange("a q n -> (a q) n").bitcast(I32))
         load_rows(w1_first, w1[:PASS, :])
         load_words(v_table[0], tab_words[0])
 
@@ -188,13 +190,13 @@ def tile_list_duplicate_collision_score_kernel(
                     out=plane[first_row + r : P : 32, :], in_=picked[64 * a + 4 * r : 64 * (a + 1) : 16, :].bitcast(I32)
                 )
 
-        w4_codes = [reorder_columns(w4_raw[:, 0, :], U16, vector_tile(2 * H, U8)[:])]
-        early_picked = vector_tile(S + PICK, U8)
+        w4_codes = [reorder_columns(w4_raw[0][:], U16, vector_tile(2 * H, U8)[:])]
+        reorder_columns(w4_rows[:], U8, early_rows[:, S + PICK :])
+        early_picked = keep.tile([P, S + PICK], U8, name="picked", align_bytes=64)
         gather(v_rows[:], idx, 0, S, U8, early_picked[:, :S])
         gather(v2_rows[:], idx2, 0, PICK, U8, early_picked[:, S:])
-        reorder_columns(w4_rows[:], U8, early_rows[:, S + PICK :])
         nc.vector.tensor_copy(early_rows[:, : S + PICK].bitcast(I32), early_picked[:].bitcast(I32))
-        w4_codes.append(reorder_columns(w4_raw[:, 1, :], U16, vector_tile(2 * H, U8)[:]))
+        late_picked = gather(v2_rows[:], idx2, PICK, S2 - PICK, U8, keep.tile([P, S2 - PICK], U8, name="picked", align_bytes=64)[:])
         v_scales = [early_planes[:, g, :].bitcast(U8)[:, :S] for g in range(2)]
         v2_scales = {(0, a): early_planes[:, a, :].bitcast(U8)[:, S : S + PICK] for a in range(2)}
         w4_moved_scales = [early_planes[:, g, :].bitcast(U8)[:, S + PICK :] for g in range(2)]
@@ -209,6 +211,8 @@ def tile_list_duplicate_collision_score_kernel(
         load_rows(w1_second[1], w1[PASS:, PASS:])
         for a in range(2):
             load_words(v2_table[a], tab2_words[a])
+        for a in range(2):
+            move_scales(late_planes, V2_PLANE_ROW[a], late_picked, a)
 
         for a in range(2):
             for u in range(2):
@@ -216,9 +220,7 @@ def tile_list_duplicate_collision_score_kernel(
         quantise_w1(0, 0, 0)
         first_pass = gather(v_table[0][:], idx, 0, S, U32)
         quantise_w1(0, 0, 1)
-        late_picked = gather(v2_rows[:], idx2, PICK, S2 - PICK, U8)
-        for a in range(2):
-            move_scales(late_planes, V2_PLANE_ROW[a], late_picked, a)
+        w4_codes.append(reorder_columns(w4_raw[1][:], U16, vector_tile(2 * H, U8)[:]))
         v_codes = {(0, half): first_pass[:, half * HALF : (half + 1) * HALF] for half in range(2)}
         for half in range(2):
             project(0, 0, half)
@@ -242,13 +244,13 @@ def tile_list_duplicate_collision_score_kernel(
         signed_weights(1, 0, 2)
         signed_weights(1, 0, 3)
         round_w1(1, 1, 1, on_vector=False)
-        round_w1(1, 1, 0, on_vector=True)
         soft_code(0, 1)
         weighted_code(0, 0)
         weighted_code(0, 1)
+        round_w1(1, 1, 0, on_vector=True)
+        quantise_h(0, 0)
         quantise_w1(1, 1, 0)
         quantise_w1(1, 1, 1)
-        quantise_h(0, 0)
         project(0, 1, 0)
         for b in range(2):
             for g in range(2):
@@ -301,6 +303,12 @@ def tile_list_duplicate_collision_score_kernel(
                     if a == 1:
                         score = stage.tile([P, S], F32, name="score")
                         rows = slice(q * PICK + n * P, q * PICK + (n + 1) * P)
+                        if 4 * q + n == S2 // P - 2:
+                            negated = vector_tile(S, F32)
+                            nc.vector.tensor_scalar(out=negated[:], in0=banks[n][:], scalar1=-1.0, scalar2=None, op0=MULT)
+                            nc.vector.tensor_tensor(out=score[:], in0=banks[n][:], in1=negated[:], op=MAX)
+                            nc.sync.dma_start(out=out[rows, :], in_=score[:])
+                            continue
                         for records in (slice(0, HALF), slice(HALF, S)) if q + n == 0 else (slice(0, S),):
                             nc.scalar.activation(score[:, records], banks[n][:, records], ACT.Abs)
                             nc.sync.dma_start(out=out[rows, records], in_=score[:, records])

@@ -21,10 +21,12 @@ P = 128
 PASS = 512
 PICK = 512
 PAIR = 2 * P
-VECTOR_TILES = 36
+VECTOR_TILES = 34
 SCALAR_TILES = 8
-WARM_PASSES = 8
-EARLY = S + PICK + H
+VECTOR_SCORES = (7, 10)
+FIRST, SECOND = 1, 0
+AHEAD = 2 * PICK
+EARLY = H + S + AHEAD
 HALF = S // 2
 V2_PLANE_ROW = (4, 8)
 
@@ -44,7 +46,7 @@ def tile_list_duplicate_collision_score_kernel(
         idx2 = lists.tile([P, S2 // 16], U16, name="idx2")
 
         v2_rows = keep.tile([P, T2 // 4], I32, name="v2_rows", align_bytes=64)
-        late_planes = keep.tile([P, (S2 - PICK) // 4], I32, name="late_planes", align_bytes=64)
+        late_planes = keep.tile([P, S2 // 4], I32, name="late_planes", align_bytes=64)
         w4_rows = keep.tile([P, H // 4], I32, name="w4_rows", align_bytes=64)
         early_rows = keep.tile([P, EARLY], U8, name="early_rows", align_bytes=64)
         v_rows = keep.tile([P, T // 4], I32, name="v_rows", align_bytes=64)
@@ -63,8 +65,8 @@ def tile_list_duplicate_collision_score_kernel(
         h_scales = keep.tile([P, 2, S], U8, name="h_scales", align_bytes=64)
 
         nc.vector.memset(w4_rows[:], 0)
-        nc.vector.memset(v2_rows[:], 0)
         nc.vector.memset(v_rows[:], 0)
+        nc.vector.memset(v2_rows[:], 0)
         nc.vector.memset(early_planes[:], 0)
         nc.vector.memset(late_planes[:], 0)
         nc.gpsimd.memset(zero_in[:], 0.0)
@@ -76,13 +78,13 @@ def tile_list_duplicate_collision_score_kernel(
         def load_words(dst, words):
             nc.sync.dma_start(out=dst[:], in_=words.rearrange("p t i -> p (t i)").bitcast(I32))
 
-        for g in range(2):
-            nc.sync.dma_start(out=w4_raw[g][:], in_=w4_words[g].bitcast(I32))
+        nc.sync.dma_start(out=w4_raw[0][:], in_=w4_words[0].bitcast(I32))
         nc.sync.dma_start(idx[:], offs)
         nc.sync.dma_start(idx2[:], offs2)
+        nc.sync.dma_start(out=gains[:], in_=gain.rearrange("(a p t) -> p a t", a=2, t=4))
         nc.sync.dma_start(out=w4_rows[0:P:4, :], in_=w4_scales.rearrange("a q n -> (a q) n").bitcast(I32))
-        nc.sync.dma_start(out=v2_rows[0:P:4, :], in_=tab2_scales.rearrange("a q n -> (a q) n").bitcast(I32))
         nc.sync.dma_start(out=v_rows[0:P:4, :], in_=tab_scales.rearrange("a q n -> (a q) n").bitcast(I32))
+        nc.sync.dma_start(out=v2_rows[0:P:4, :], in_=tab2_scales.rearrange("a q n -> (a q) n").bitcast(I32))
         load_rows(w1_first, w1[:PASS, :])
         load_words(v_table[0], tab_words[0])
 
@@ -156,7 +158,7 @@ def tile_list_duplicate_collision_score_kernel(
                 first = a * PASS + t * P
                 nc.tensor.matmul_mx(
                     out=c_bank[a, b][:, t, :],
-                    lhsT=w4_codes[g][:, 2 * first : 2 * (first + P)].bitcast(FP4X4),
+                    lhsT=w4_codes[g, a][:, 2 * t * P : 2 * (t + 1) * P].bitcast(FP4X4),
                     lhsT_scale=w4_moved_scales[g][:, first : first + P],
                     rhs=v_codes[g, b // 2][:, (b % 2) * P : (b % 2 + 1) * P].bitcast(FP8X4),
                     rhs_scale=v_scales[g][:, records],
@@ -190,125 +192,138 @@ def tile_list_duplicate_collision_score_kernel(
                     out=plane[first_row + r : P : 32, :], in_=picked[64 * a + 4 * r : 64 * (a + 1) : 16, :].bitcast(I32)
                 )
 
-        w4_codes = [reorder_columns(w4_raw[0][:], U16, vector_tile(2 * H, U8)[:])]
-        reorder_columns(w4_rows[:], U8, early_rows[:, S + PICK :])
-        early_picked = keep.tile([P, S + PICK], U8, name="picked", align_bytes=64)
-        gather(v_rows[:], idx, 0, S, U8, early_picked[:, :S])
-        gather(v2_rows[:], idx2, 0, PICK, U8, early_picked[:, S:])
-        nc.vector.tensor_copy(early_rows[:, : S + PICK].bitcast(I32), early_picked[:].bitcast(I32))
-        late_picked = gather(v2_rows[:], idx2, PICK, S2 - PICK, U8, keep.tile([P, S2 - PICK], U8, name="picked", align_bytes=64)[:])
-        v_scales = [early_planes[:, g, :].bitcast(U8)[:, :S] for g in range(2)]
-        v2_scales = {(0, a): early_planes[:, a, :].bitcast(U8)[:, S : S + PICK] for a in range(2)}
-        w4_moved_scales = [early_planes[:, g, :].bitcast(U8)[:, S + PICK :] for g in range(2)]
-        for q in range(1, S2 // PICK):
-            for a in range(2):
-                v2_scales[q, a] = late_planes[V2_PLANE_ROW[a] :, :].bitcast(U8)[:, (q - 1) * PICK : q * PICK]
-        move_scales(early_planes[:, 0, :], 0, early_rows, 0)
-        load_rows(w1_second[0], w1[PASS:, :PASS])
-        nc.sync.dma_start(out=gains[:], in_=gain.rearrange("(a p t) -> p a t", a=2, t=4))
-        move_scales(early_planes[:, 1, :], 0, early_rows, 1)
+        first_words = reorder_columns(w4_raw[0][:], U16, vector_tile(2 * H, U8)[:])
+        w4_codes = {(0, a): first_words[:, 2 * a * PASS : 2 * (a + 1) * PASS] for a in range(2)}
+        reorder_columns(w4_rows[:], U8, early_rows[:, :H])
+        v_picked = gather(v_rows[:], idx, 0, S, U8, keep.tile([P, S], U8, name="picked", align_bytes=64)[:])
+        nc.vector.tensor_copy(early_rows[:, H : H + S].bitcast(I32), v_picked.bitcast(I32))
+        move_scales(early_planes[:, 0, : (H + S) // 4], 0, early_rows[:, : H + S], 0)
+        v2_picked = gather(v2_rows[:], idx2, 0, S2, U8, keep.tile([P, S2], U8, name="picked", align_bytes=64)[:])
+        nc.vector.tensor_copy(early_rows[:, H + S :].bitcast(I32), v2_picked[:, :AHEAD].bitcast(I32))
+        w4_moved_scales = [early_planes[:, g, :].bitcast(U8)[:, :H] for g in range(2)]
+        v_scales = [early_planes[:, g, :].bitcast(U8)[:, H : H + S] for g in range(2)]
+        v2_scales = {}
+        for q in range(S2 // PICK):
+            columns = slice(q * PICK, (q + 1) * PICK)
+            v2_scales[q, SECOND] = late_planes[V2_PLANE_ROW[0] :, :].bitcast(U8)[:, columns]
+            if q * PICK < AHEAD:
+                v2_scales[q, FIRST] = early_planes[:, FIRST, :].bitcast(U8)[:, H + S :][:, columns]
+            else:
+                v2_scales[q, FIRST] = late_planes[V2_PLANE_ROW[1] :, :].bitcast(U8)[:, columns]
+        load_rows(w1_second[FIRST], w1[PASS:, FIRST * PASS : (FIRST + 1) * PASS])
         load_words(v_table[1], tab_words[1])
-        load_rows(w1_second[1], w1[PASS:, PASS:])
-        for a in range(2):
+        move_scales(early_planes[:, 1, :], 0, early_rows, 1)
+        nc.sync.dma_start(out=w4_raw[1][:], in_=w4_words[1].bitcast(I32))
+        load_rows(w1_second[SECOND], w1[PASS:, SECOND * PASS : (SECOND + 1) * PASS])
+        for a in (FIRST, SECOND):
             load_words(v2_table[a], tab2_words[a])
-        for a in range(2):
-            move_scales(late_planes, V2_PLANE_ROW[a], late_picked, a)
+        move_scales(late_planes, V2_PLANE_ROW[0], v2_picked, SECOND)
+        move_scales(late_planes[:, AHEAD // 4 :], V2_PLANE_ROW[1], v2_picked[:, AHEAD:], FIRST)
 
-        for a in range(2):
+        for a in (FIRST, SECOND):
             for u in range(2):
                 round_w1(0, a, u, on_vector=False)
-        quantise_w1(0, 0, 0)
+        quantise_w1(0, FIRST, 0)
         first_pass = gather(v_table[0][:], idx, 0, S, U32)
-        quantise_w1(0, 0, 1)
-        w4_codes.append(reorder_columns(w4_raw[1][:], U16, vector_tile(2 * H, U8)[:]))
+        quantise_w1(0, FIRST, 1)
         v_codes = {(0, half): first_pass[:, half * HALF : (half + 1) * HALF] for half in range(2)}
         for half in range(2):
-            project(0, 0, half)
+            project(0, FIRST, half)
         for b in range(4):
-            signed_weights(0, 0, b)
+            signed_weights(0, FIRST, b)
 
-        round_w1(1, 0, 0, on_vector=True)
-        round_w1(1, 0, 1, on_vector=False)
-        quantise_w1(0, 1, 0)
-        quantise_w1(1, 0, 0)
-        quantise_w1(1, 0, 1)
-        quantise_w1(0, 1, 1)
+        round_w1(1, FIRST, 0, on_vector=True)
+        round_w1(1, FIRST, 1, on_vector=False)
+        quantise_w1(0, SECOND, 0)
+        quantise_w1(1, FIRST, 0)
+        quantise_w1(1, FIRST, 1)
+        quantise_w1(0, SECOND, 1)
         for half in range(2):
             v_codes[1, half] = gather(v_table[1][:], idx, half * HALF, HALF, U32)
+        for a in (FIRST, SECOND):
+            words = w4_raw[1][:, a * PASS // 2 : (a + 1) * PASS // 2]
+            w4_codes[1, a] = reorder_columns(words, U16, vector_tile(2 * PASS, U8)[:])
 
-        project(1, 0, 0)
-        soft_code(0, 0)
-        signed_weights(1, 0, 0)
-        signed_weights(1, 0, 1)
-        project(1, 0, 1)
-        signed_weights(1, 0, 2)
-        signed_weights(1, 0, 3)
-        round_w1(1, 1, 1, on_vector=False)
-        soft_code(0, 1)
-        weighted_code(0, 0)
-        weighted_code(0, 1)
-        round_w1(1, 1, 0, on_vector=True)
-        quantise_h(0, 0)
-        quantise_w1(1, 1, 0)
-        quantise_w1(1, 1, 1)
-        project(0, 1, 0)
-        for b in range(2):
-            for g in range(2):
-                signed_weights(g, 1, b)
-        project(1, 1, 0)
-        soft_code(1, 0)
-        weighted_code(0, 2)
-        weighted_code(0, 3)
+        project(1, FIRST, 0)
+        soft_code(FIRST, 0)
+        signed_weights(1, FIRST, 0)
+        signed_weights(1, FIRST, 1)
+        project(1, FIRST, 1)
+        signed_weights(1, FIRST, 2)
+        signed_weights(1, FIRST, 3)
+        soft_code(FIRST, 1)
+        round_w1(1, SECOND, 1, on_vector=False)
+        weighted_code(FIRST, 0)
+        weighted_code(FIRST, 1)
+        round_w1(1, SECOND, 0, on_vector=True)
+        weighted_code(FIRST, 2)
+        for u in range(2):
+            quantise_w1(1, SECOND, u)
+        weighted_code(FIRST, 3)
+        project(0, SECOND, 0)
         for g in range(2):
-            project(g, 1, 1)
-        soft_code(1, 1)
+            signed_weights(g, SECOND, 0)
+        project(1, SECOND, 0)
+        soft_code(SECOND, 0)
+        for g in range(2):
+            signed_weights(g, SECOND, 1)
+        for g in range(2):
+            project(g, SECOND, 1)
+        soft_code(SECOND, 1)
         for b in range(2, 4):
             for g in range(2):
-                signed_weights(g, 1, b)
-        quantise_h(0, 1)
-        weighted_code(1, 0)
-        weighted_code(1, 1)
-        pick_v2_words(0, 0)
-        weighted_code(1, 2)
-        weighted_code(1, 3)
+                signed_weights(g, SECOND, b)
         for half in range(2):
-            quantise_h(1, half)
-        pick_v2_words(0, 1)
+            quantise_h(FIRST, half)
+        weighted_code(SECOND, 0)
+        weighted_code(SECOND, 1)
+        pick_v2_words(0, FIRST)
+        weighted_code(SECOND, 2)
+        weighted_code(SECOND, 3)
+        pick_v2_words(1, FIRST)
+        for half in range(2):
+            quantise_h(SECOND, half)
 
-        def score_pass(bank, q, a, n, half, start, stop, codes_of=None):
-            records = slice(half * HALF, (half + 1) * HALF)
-            nc.tensor.matmul_mx(
-                out=bank[:, records],
-                lhsT=v2_codes[q, a][:, n * P : (n + 1) * P].bitcast(FP8X4),
-                lhsT_scale=v2_scales[q, a][:, n * P : (n + 1) * P],
-                rhs=h_codes[a if codes_of is None else codes_of, half][:].bitcast(FP8X4),
-                rhs_scale=h_scales[:, a if codes_of is None else codes_of, records],
-                start=start,
-                stop=stop,
-            )
+        score_banks = [psum.tile([P, S], F32, name="bank%d" % (tile % 8)) for tile in range(S2 // P)]
 
-        score_banks = [psum.tile([P, S], F32, name="bank%d" % (n % 8)) for n in range(S2 // P)]
-        for q in range(S2 // PICK):
-            for a in range(2):
-                if (q, a) not in v2_codes:
-                    pick_v2_words(q, a)
-            banks = score_banks[4 * q : 4 * q + 4]
-            for a in range(2):
-                if q == 0 and a == 1:
-                    for repeat in range(WARM_PASSES):
-                        score_pass(score_banks[7], 0, 0, 0, 1, True, True, codes_of=1)
-                for n in range(4):
-                    for half in range(2):
-                        score_pass(banks[n], q, a, n, half, a == 0 and half == 0, a == 1 and half == 1)
-                    if a == 1:
-                        score = stage.tile([P, S], F32, name="score")
-                        rows = slice(q * PICK + n * P, q * PICK + (n + 1) * P)
-                        if 4 * q + n == S2 // P - 2:
-                            negated = vector_tile(S, F32)
-                            nc.vector.tensor_scalar(out=negated[:], in0=banks[n][:], scalar1=-1.0, scalar2=None, op0=MULT)
-                            nc.vector.tensor_tensor(out=score[:], in0=banks[n][:], in1=negated[:], op=MAX)
-                            nc.sync.dma_start(out=out[rows, :], in_=score[:])
-                            continue
-                        for records in (slice(0, HALF), slice(HALF, S)) if q + n == 0 else (slice(0, S),):
-                            nc.scalar.activation(score[:, records], banks[n][:, records], ACT.Abs)
-                            nc.sync.dma_start(out=out[rows, records], in_=score[:, records])
+        def score_pass(tile, a):
+            q, n = divmod(tile, 4)
+            for half in range(2):
+                records = slice(half * HALF, (half + 1) * HALF)
+                nc.tensor.matmul_mx(
+                    out=score_banks[tile][:, records],
+                    lhsT=v2_codes[q, a][:, n * P : (n + 1) * P].bitcast(FP8X4),
+                    lhsT_scale=v2_scales[q, a][:, n * P : (n + 1) * P],
+                    rhs=h_codes[a, half][:].bitcast(FP8X4),
+                    rhs_scale=h_scales[:, a, records],
+                    start=(a == FIRST and half == 0),
+                    stop=(a == SECOND and half == 1),
+                )
+
+        def store_scores(tile):
+            score = stage.tile([P, S], F32, name="score")
+            rows = slice(tile * P, (tile + 1) * P)
+            if tile in VECTOR_SCORES:
+                negated = vector_tile(S, F32)
+                nc.vector.tensor_scalar(out=negated[:], in0=score_banks[tile][:], scalar1=-1.0, scalar2=None, op0=MULT)
+                nc.vector.tensor_tensor(out=score[:], in0=score_banks[tile][:], in1=negated[:], op=MAX)
+                nc.sync.dma_start(out=out[rows, :], in_=score[:])
+                return
+            for records in (slice(0, HALF), slice(HALF, S)) if tile == 0 else (slice(0, S),):
+                nc.scalar.activation(score[:, records], score_banks[tile][:, records], ACT.Abs)
+                nc.sync.dma_start(out=out[rows, records], in_=score[:, records])
+
+        for tile in range(8):
+            score_pass(tile, FIRST)
+        for q in range(2):
+            pick_v2_words(q, SECOND)
+        for a in (FIRST, SECOND):
+            pick_v2_words(2, a)
+        for tile in range(8):
+            score_pass(tile, SECOND)
+            store_scores(tile)
+        for tile in range(8, 12):
+            score_pass(tile, FIRST)
+        for tile in range(8, 12):
+            score_pass(tile, SECOND)
+            store_scores(tile)

@@ -15,20 +15,15 @@ FP8X4 = mybir.dt.float8_e4m3fn_x4
 FP4X4 = mybir.dt.float4_e2m1fn_x4
 ACT = mybir.ActivationFunctionType
 MULT = mybir.AluOpType.mult
-MAX = mybir.AluOpType.max
 
 P = 128
 PASS = 512
-PICK = 512
 PAIR = 2 * P
-VECTOR_TILES = 34
-SCALAR_TILES = 8
-VECTOR_SCORES = (7, 10)
-FIRST, SECOND = 1, 0
-AHEAD = 2 * PICK
-EARLY = H + S + AHEAD
 HALF = S // 2
-V2_PLANE_ROW = (4, 8)
+FIRST, SECOND = 1, 0
+AHEAD = 2
+VECTOR_TILES = 34
+SCALAR_TILES = 15
 
 
 def tile_list_duplicate_collision_score_kernel(
@@ -45,14 +40,17 @@ def tile_list_duplicate_collision_score_kernel(
         idx = lists.tile([P, S // 16], U16, name="idx")
         idx2 = lists.tile([P, S2 // 16], U16, name="idx2")
 
-        v2_rows = keep.tile([P, T2 // 4], I32, name="v2_rows", align_bytes=64)
-        late_planes = keep.tile([P, S2 // 4], I32, name="late_planes", align_bytes=64)
-        w4_rows = keep.tile([P, H // 4], I32, name="w4_rows", align_bytes=64)
-        early_rows = keep.tile([P, EARLY], U8, name="early_rows", align_bytes=64)
         v_rows = keep.tile([P, T // 4], I32, name="v_rows", align_bytes=64)
-        early_planes = keep.tile([P, 2, EARLY // 4], I32, name="early_planes", align_bytes=64)
-        w4_raw = [keep.tile([P, H // 2], I32, name="w4_raw%d" % g, align_bytes=64) for g in range(2)]
-        gains = keep.tile([P, 2, 4], F32, name="gains")
+        w4_rows = keep.tile([P, H // 4], I32, name="w4_rows", align_bytes=64)
+        v2_rows = keep.tile([P, T2 // 4], I32, name="v2_rows", align_bytes=64)
+        joined_rows = keep.tile([P, H + S + S2], U8, name="joined_rows", align_bytes=64)
+        planes = {
+            SECOND: keep.tile([P, (H + S) // 4], I32, name="planes_second", align_bytes=64),
+            FIRST: keep.tile([P, (H + S + S2) // 4], I32, name="planes_first", align_bytes=64),
+        }
+        last_plane = keep.tile([P, S2 // 4], I32, name="last_plane", align_bytes=64)
+        w4_raw = keep.tile([P, 2, H // 2], I32, name="w4_raw", align_bytes=64)
+        gains = keep.tile([P, 2, 8], F32, name="gains")
         zero_in = keep.tile([P, 1], F32, name="zero_in")
         zero = keep.tile([P, 1], F32, name="zero")
         w1_first = keep.tile([P, 4, H], F32, name="w1_first")
@@ -64,11 +62,8 @@ def tile_list_duplicate_collision_score_kernel(
         w1_scales = keep.tile([P, 2 * H], U8, name="w1_scales", align_bytes=64)
         h_scales = keep.tile([P, 2, S], U8, name="h_scales", align_bytes=64)
 
-        nc.vector.memset(w4_rows[:], 0)
-        nc.vector.memset(v_rows[:], 0)
-        nc.vector.memset(v2_rows[:], 0)
-        nc.vector.memset(early_planes[:], 0)
-        nc.vector.memset(late_planes[:], 0)
+        for cleared in (v_rows, w4_rows, v2_rows, planes[0], planes[1], last_plane):
+            nc.vector.memset(cleared[:], 0)
         nc.gpsimd.memset(zero_in[:], 0.0)
         nc.scalar.activation(zero[:], zero_in[:], ACT.Tanh)
 
@@ -78,38 +73,46 @@ def tile_list_duplicate_collision_score_kernel(
         def load_words(dst, words):
             nc.sync.dma_start(out=dst[:], in_=words.rearrange("p t i -> p (t i)").bitcast(I32))
 
-        nc.sync.dma_start(out=w4_raw[0][:], in_=w4_words[0].bitcast(I32))
+        def load_scale_rows(dst, scales):
+            nc.sync.dma_start(out=dst[0:P:4, :], in_=scales.rearrange("a q n -> (a q) n").bitcast(I32))
+
+        nc.sync.dma_start(out=w4_raw[:], in_=w4_words.rearrange("a p n -> p a n").bitcast(I32))
         nc.sync.dma_start(idx[:], offs)
+        load_scale_rows(v_rows, tab_scales)
+        load_scale_rows(w4_rows, w4_scales)
         nc.sync.dma_start(idx2[:], offs2)
-        nc.sync.dma_start(out=gains[:], in_=gain.rearrange("(a p t) -> p a t", a=2, t=4))
-        nc.sync.dma_start(out=w4_rows[0:P:4, :], in_=w4_scales.rearrange("a q n -> (a q) n").bitcast(I32))
-        nc.sync.dma_start(out=v_rows[0:P:4, :], in_=tab_scales.rearrange("a q n -> (a q) n").bitcast(I32))
-        nc.sync.dma_start(out=v2_rows[0:P:4, :], in_=tab2_scales.rearrange("a q n -> (a q) n").bitcast(I32))
+        nc.sync.dma_start(out=gains[:, :, :4], in_=gain.rearrange("(a p t) -> p a t", a=2, t=4))
+        load_scale_rows(v2_rows, tab2_scales)
         load_rows(w1_first, w1[:PASS, :])
         load_words(v_table[0], tab_words[0])
 
         def vector_tile(width, dtype):
             return ordered.tile([P, width], dtype, name="vector_out", align_bytes=64, bufs=VECTOR_TILES)
 
-        def scalar_tile(shape, dtype):
-            return ordered.tile(shape, dtype, name="scalar_out", align_bytes=64, bufs=SCALAR_TILES)
+        def scalar_tile(width, dtype):
+            return ordered.tile([P, width], dtype, name="scalar_out", align_bytes=64, bufs=SCALAR_TILES)
 
         def gather(window, offsets, first, count, dtype, picked=None):
             picked = vector_tile(count, dtype)[:] if picked is None else picked
             nc.vector.tensor_copy(picked, window.bitcast(dtype).indirect(offsets[:, first // 16 : (first + count) // 16]))
             return picked
 
-        def reorder_columns(raw, dtype, moved):
-            nc.vector.tensor_copy(
+        def reorder_columns(copy, raw, dtype, moved):
+            copy(
                 out=moved.bitcast(dtype).rearrange("p (b t m) -> p b t m", t=4, m=P),
                 in_=raw.bitcast(dtype).rearrange("p (b m t) -> p b t m", t=4, m=P),
             )
             return moved
 
-        rounded, w1_codes, p_bank, tanh_p, c_bank, h_rounded, h_codes, v2_codes = {}, {}, {}, {}, {}, {}, {}, {}
+        def move_scales(plane, picked, a):
+            for r in range(4):
+                nc.sync.dma_start(out=plane[r:P:32, :], in_=picked[64 * a + 4 * r : 64 * (a + 1) : 16, :].bitcast(I32))
+
+        rounded, w1_codes, v_codes, v2_codes = {}, {}, {}, {}
+        p_bank, c_bank, tanh_p, h_rounded, h_codes = {}, {}, {}, {}, {}
 
         def round_w1(g, a, u, on_vector):
-            rounded[g, a, u] = vector_tile(4 * PAIR, BF16) if on_vector else scalar_tile([P, 4 * PAIR], BF16)
+            rounded[g, a, u] = (vector_tile if on_vector else scalar_tile)(4 * PAIR, BF16)
             copy = nc.vector.tensor_copy if on_vector else nc.scalar.copy
             copy(
                 out=rounded[g, a, u][:].rearrange("p (e m j) -> p m j e", e=2, j=4),
@@ -138,32 +141,30 @@ def tile_list_duplicate_collision_score_kernel(
                     stop=(g == 1 and t % 2 == 1),
                 )
 
-        def soft_code(a, half):
-            tanh_p[a, half] = scalar_tile([P, 4, HALF], F32)
-            for first in range(0, HALF, P):
-                for t in range(4):
-                    nc.scalar.activation(
-                        tanh_p[a, half][:, t, first : first + P],
-                        p_bank[a, half, t // 2][:, t % 2, first : first + P],
-                        ACT.Tanh,
-                        bias=zero[:],
-                        scale=gains[:, a, t : t + 1],
-                    )
-
         def signed_weights(g, a, b):
-            records = slice(b * P, (b + 1) * P)
             if g == 0:
                 c_bank[a, b] = psum.tile([P, 4, P], F32, name="bank%d" % (4 + b))
             for t in range(4):
                 first = a * PASS + t * P
                 nc.tensor.matmul_mx(
                     out=c_bank[a, b][:, t, :],
-                    lhsT=w4_codes[g, a][:, 2 * t * P : 2 * (t + 1) * P].bitcast(FP4X4),
+                    lhsT=w4_codes[g][:, 2 * first : 2 * (first + P)].bitcast(FP4X4),
                     lhsT_scale=w4_moved_scales[g][:, first : first + P],
                     rhs=v_codes[g, b // 2][:, (b % 2) * P : (b % 2 + 1) * P].bitcast(FP8X4),
-                    rhs_scale=v_scales[g][:, records],
+                    rhs_scale=v_scales[g][:, b * P : (b + 1) * P],
                     start=(g == 0 and t == 0),
                     stop=(g == 1 and t == 3),
+                )
+
+        def soft_code(a, b):
+            tanh_p[a, b] = scalar_tile(4 * P, F32)
+            for t in range(4):
+                nc.scalar.activation(
+                    tanh_p[a, b][:, t * P : (t + 1) * P],
+                    p_bank[a, b // 2, t // 2][:, t % 2, (b % 2) * P : (b % 2 + 1) * P],
+                    ACT.Tanh,
+                    bias=zero[:],
+                    scale=gains[:, a, t : t + 1],
                 )
 
         def weighted_code(a, b):
@@ -172,61 +173,48 @@ def tile_list_duplicate_collision_score_kernel(
             nc.vector.tensor_tensor(
                 out=h_rounded[a, b // 2][:, (b % 2) * 4 * P : (b % 2 + 1) * 4 * P].rearrange("p (n i t) -> p n t i", i=2, t=4),
                 in0=c_bank[a, b][:].rearrange("p t (n i) -> p n t i", i=2),
-                in1=tanh_p[a, b // 2][:, :, (b % 2) * P : (b % 2 + 1) * P].rearrange("p t (n i) -> p n t i", i=2),
+                in1=tanh_p[a, b][:].rearrange("p (t n i) -> p n t i", t=4, i=2),
                 op=MULT,
             )
 
         def quantise_h(a, half):
-            records = slice(half * HALF, (half + 1) * HALF)
             h_codes[a, half] = vector_tile(HALF, U32)
             nc.vector.quantize_mx(
-                out=h_codes[a, half][:].bitcast(FP8X4), scales=h_scales[:, a, records], in_=h_rounded[a, half][:]
+                out=h_codes[a, half][:].bitcast(FP8X4),
+                scales=h_scales[:, a, half * HALF : (half + 1) * HALF],
+                in_=h_rounded[a, half][:],
             )
 
-        def pick_v2_words(q, a):
-            v2_codes[q, a] = gather(v2_table[a][:], idx2, q * PICK, PICK, U32)
+        def pick_v2_words(a, q):
+            v2_codes[a, q] = gather(v2_table[a][:], idx2, q * PAIR, PAIR, U32)
 
-        def move_scales(plane, first_row, picked, a):
-            for r in range(4):
-                nc.sync.dma_start(
-                    out=plane[first_row + r : P : 32, :], in_=picked[64 * a + 4 * r : 64 * (a + 1) : 16, :].bitcast(I32)
-                )
-
-        first_words = reorder_columns(w4_raw[0][:], U16, vector_tile(2 * H, U8)[:])
-        w4_codes = {(0, a): first_words[:, 2 * a * PASS : 2 * (a + 1) * PASS] for a in range(2)}
-        reorder_columns(w4_rows[:], U8, early_rows[:, :H])
+        w4_codes = [reorder_columns(nc.scalar.copy, w4_raw[:, g, :], U16, scalar_tile(2 * H, U8)[:]) for g in range(2)]
         v_picked = gather(v_rows[:], idx, 0, S, U8, keep.tile([P, S], U8, name="picked", align_bytes=64)[:])
-        nc.vector.tensor_copy(early_rows[:, H : H + S].bitcast(I32), v_picked.bitcast(I32))
-        move_scales(early_planes[:, 0, : (H + S) // 4], 0, early_rows[:, : H + S], 0)
+        reorder_columns(nc.vector.tensor_copy, w4_rows[:], U8, joined_rows[:, :H])
+        nc.vector.tensor_copy(joined_rows[:, H : H + S].bitcast(I32), v_picked.bitcast(I32))
+        move_scales(planes[0], joined_rows[:, : H + S], 0)
         v2_picked = gather(v2_rows[:], idx2, 0, S2, U8, keep.tile([P, S2], U8, name="picked", align_bytes=64)[:])
-        nc.vector.tensor_copy(early_rows[:, H + S :].bitcast(I32), v2_picked[:, :AHEAD].bitcast(I32))
-        w4_moved_scales = [early_planes[:, g, :].bitcast(U8)[:, :H] for g in range(2)]
-        v_scales = [early_planes[:, g, :].bitcast(U8)[:, H : H + S] for g in range(2)]
-        v2_scales = {}
-        for q in range(S2 // PICK):
-            columns = slice(q * PICK, (q + 1) * PICK)
-            v2_scales[q, SECOND] = late_planes[V2_PLANE_ROW[0] :, :].bitcast(U8)[:, columns]
-            if q * PICK < AHEAD:
-                v2_scales[q, FIRST] = early_planes[:, FIRST, :].bitcast(U8)[:, H + S :][:, columns]
-            else:
-                v2_scales[q, FIRST] = late_planes[V2_PLANE_ROW[1] :, :].bitcast(U8)[:, columns]
+        nc.vector.tensor_copy(joined_rows[:, H + S :].bitcast(I32), v2_picked.bitcast(I32))
+        w4_moved_scales = [planes[g][:].bitcast(U8)[:, :H] for g in range(2)]
+        v_scales = [planes[g][:].bitcast(U8)[:, H : H + S] for g in range(2)]
+        v2_scales = {FIRST: planes[FIRST][:].bitcast(U8)[:, H + S :], SECOND: last_plane[:].bitcast(U8)}
         load_rows(w1_second[FIRST], w1[PASS:, FIRST * PASS : (FIRST + 1) * PASS])
         load_words(v_table[1], tab_words[1])
-        move_scales(early_planes[:, 1, :], 0, early_rows, 1)
-        nc.sync.dma_start(out=w4_raw[1][:], in_=w4_words[1].bitcast(I32))
+        move_scales(planes[1], joined_rows, 1)
         load_rows(w1_second[SECOND], w1[PASS:, SECOND * PASS : (SECOND + 1) * PASS])
         for a in (FIRST, SECOND):
             load_words(v2_table[a], tab2_words[a])
-        move_scales(late_planes, V2_PLANE_ROW[0], v2_picked, SECOND)
-        move_scales(late_planes[:, AHEAD // 4 :], V2_PLANE_ROW[1], v2_picked[:, AHEAD:], FIRST)
+        move_scales(last_plane, v2_picked, SECOND)
 
-        for a in (FIRST, SECOND):
-            for u in range(2):
-                round_w1(0, a, u, on_vector=False)
+        round_w1(0, FIRST, 0, on_vector=False)
+        round_w1(0, FIRST, 1, on_vector=False)
+        round_w1(0, SECOND, 1, on_vector=False)
         quantise_w1(0, FIRST, 0)
+        round_w1(0, SECOND, 0, on_vector=True)
         first_pass = gather(v_table[0][:], idx, 0, S, U32)
+        v_codes.update({(0, half): first_pass[:, half * HALF : (half + 1) * HALF] for half in range(2)})
         quantise_w1(0, FIRST, 1)
-        v_codes = {(0, half): first_pass[:, half * HALF : (half + 1) * HALF] for half in range(2)}
+        quantise_w1(0, SECOND, 0)
         for half in range(2):
             project(0, FIRST, half)
         for b in range(4):
@@ -234,96 +222,86 @@ def tile_list_duplicate_collision_score_kernel(
 
         round_w1(1, FIRST, 0, on_vector=True)
         round_w1(1, FIRST, 1, on_vector=False)
-        quantise_w1(0, SECOND, 0)
+        quantise_w1(0, SECOND, 1)
         quantise_w1(1, FIRST, 0)
         quantise_w1(1, FIRST, 1)
-        quantise_w1(0, SECOND, 1)
         for half in range(2):
             v_codes[1, half] = gather(v_table[1][:], idx, half * HALF, HALF, U32)
-        for a in (FIRST, SECOND):
-            words = w4_raw[1][:, a * PASS // 2 : (a + 1) * PASS // 2]
-            w4_codes[1, a] = reorder_columns(words, U16, vector_tile(2 * PASS, U8)[:])
+        for half in range(2):
+            project(1, FIRST, half)
+            signed_weights(1, FIRST, 2 * half)
+            signed_weights(1, FIRST, 2 * half + 1)
 
-        project(1, FIRST, 0)
-        soft_code(FIRST, 0)
-        signed_weights(1, FIRST, 0)
-        signed_weights(1, FIRST, 1)
-        project(1, FIRST, 1)
-        signed_weights(1, FIRST, 2)
-        signed_weights(1, FIRST, 3)
-        soft_code(FIRST, 1)
+        for b in range(2):
+            soft_code(FIRST, b)
+            weighted_code(FIRST, b)
         round_w1(1, SECOND, 1, on_vector=False)
-        weighted_code(FIRST, 0)
-        weighted_code(FIRST, 1)
         round_w1(1, SECOND, 0, on_vector=True)
-        weighted_code(FIRST, 2)
+        quantise_h(FIRST, 0)
         for u in range(2):
             quantise_w1(1, SECOND, u)
-        weighted_code(FIRST, 3)
+        for b in range(2, 4):
+            soft_code(FIRST, b)
+            weighted_code(FIRST, b)
+
         project(0, SECOND, 0)
-        for g in range(2):
-            signed_weights(g, SECOND, 0)
+        for b in range(2):
+            for g in range(2):
+                signed_weights(g, SECOND, b)
         project(1, SECOND, 0)
-        soft_code(SECOND, 0)
-        for g in range(2):
-            signed_weights(g, SECOND, 1)
         for g in range(2):
             project(g, SECOND, 1)
-        soft_code(SECOND, 1)
         for b in range(2, 4):
             for g in range(2):
                 signed_weights(g, SECOND, b)
-        for half in range(2):
-            quantise_h(FIRST, half)
-        weighted_code(SECOND, 0)
-        weighted_code(SECOND, 1)
-        pick_v2_words(0, FIRST)
-        weighted_code(SECOND, 2)
-        weighted_code(SECOND, 3)
-        pick_v2_words(1, FIRST)
-        for half in range(2):
-            quantise_h(SECOND, half)
+        for b in range(4):
+            soft_code(SECOND, b)
+            weighted_code(SECOND, b)
+            if b == 0:
+                quantise_h(FIRST, 1)
+            if b == 2:
+                quantise_h(SECOND, 0)
+        pick_v2_words(FIRST, 0)
+        quantise_h(SECOND, 1)
+        for q in range(1, AHEAD):
+            pick_v2_words(FIRST, q)
 
-        score_banks = [psum.tile([P, S], F32, name="bank%d" % (tile % 8)) for tile in range(S2 // P)]
+        score_banks = {(0, half): psum.tile([P, HALF], F32, name="bank%d" % (half * 2 * AHEAD))[:] for half in range(2)}
+        for tile in range(1, S2 // P):
+            bank = psum.tile([P, S], F32, name="bank%d" % (tile % (2 * AHEAD)))
+            score_banks.update({(tile, half): bank[:, half * HALF : (half + 1) * HALF] for half in range(2)})
+            score_banks[tile, "whole"] = bank[:]
 
         def score_pass(tile, a):
-            q, n = divmod(tile, 4)
+            q, n = divmod(tile, 2)
             for half in range(2):
                 records = slice(half * HALF, (half + 1) * HALF)
                 nc.tensor.matmul_mx(
-                    out=score_banks[tile][:, records],
-                    lhsT=v2_codes[q, a][:, n * P : (n + 1) * P].bitcast(FP8X4),
-                    lhsT_scale=v2_scales[q, a][:, n * P : (n + 1) * P],
+                    out=score_banks[tile, half],
+                    lhsT=v2_codes[a, q][:, n * P : (n + 1) * P].bitcast(FP8X4),
+                    lhsT_scale=v2_scales[a][:, tile * P : (tile + 1) * P],
                     rhs=h_codes[a, half][:].bitcast(FP8X4),
                     rhs_scale=h_scales[:, a, records],
-                    start=(a == FIRST and half == 0),
-                    stop=(a == SECOND and half == 1),
+                    start=(a == FIRST and (half == 0 or tile == 0)),
+                    stop=(a == SECOND and (half == 1 or tile == 0)),
                 )
 
         def store_scores(tile):
             score = stage.tile([P, S], F32, name="score")
             rows = slice(tile * P, (tile + 1) * P)
-            if tile in VECTOR_SCORES:
-                negated = vector_tile(S, F32)
-                nc.vector.tensor_scalar(out=negated[:], in0=score_banks[tile][:], scalar1=-1.0, scalar2=None, op0=MULT)
-                nc.vector.tensor_tensor(out=score[:], in0=score_banks[tile][:], in1=negated[:], op=MAX)
-                nc.sync.dma_start(out=out[rows, :], in_=score[:])
-                return
-            for records in (slice(0, HALF), slice(HALF, S)) if tile == 0 else (slice(0, S),):
-                nc.scalar.activation(score[:, records], score_banks[tile][:, records], ACT.Abs)
+            parts = {0: slice(0, HALF), 1: slice(HALF, S)} if tile == 0 else {"whole": slice(0, S)}
+            for part, records in parts.items():
+                nc.scalar.activation(score[:, records], score_banks[tile, part], ACT.Abs)
                 nc.sync.dma_start(out=out[rows, records], in_=score[:, records])
 
-        for tile in range(8):
+        for tile in range(2 * AHEAD):
             score_pass(tile, FIRST)
-        for q in range(2):
-            pick_v2_words(q, SECOND)
-        for a in (FIRST, SECOND):
-            pick_v2_words(2, a)
-        for tile in range(8):
-            score_pass(tile, SECOND)
-            store_scores(tile)
-        for tile in range(8, 12):
-            score_pass(tile, FIRST)
-        for tile in range(8, 12):
-            score_pass(tile, SECOND)
-            store_scores(tile)
+        for q in range(S2 // PAIR):
+            if q >= AHEAD:
+                pick_v2_words(FIRST, q)
+            pick_v2_words(SECOND, q)
+            for tile in (2 * q, 2 * q + 1):
+                if q >= AHEAD:
+                    score_pass(tile, FIRST)
+                score_pass(tile, SECOND)
+                store_scores(tile)

@@ -22,6 +22,8 @@ PAIR = 2 * P
 HALF = S // 2
 FIRST, SECOND = 1, 0
 AHEAD = 2
+EARLY = AHEAD * PAIR
+LATE_ROW = 4
 VECTOR_TILES = 34
 SCALAR_TILES = 15
 
@@ -43,10 +45,10 @@ def tile_list_duplicate_collision_score_kernel(
         v_rows = keep.tile([P, T // 4], I32, name="v_rows", align_bytes=64)
         w4_rows = keep.tile([P, H // 4], I32, name="w4_rows", align_bytes=64)
         v2_rows = keep.tile([P, T2 // 4], I32, name="v2_rows", align_bytes=64)
-        joined_rows = keep.tile([P, H + S + S2], U8, name="joined_rows", align_bytes=64)
+        joined_rows = keep.tile([P, H + S + EARLY], U8, name="joined_rows", align_bytes=64)
         planes = {
             SECOND: keep.tile([P, (H + S) // 4], I32, name="planes_second", align_bytes=64),
-            FIRST: keep.tile([P, (H + S + S2) // 4], I32, name="planes_first", align_bytes=64),
+            FIRST: keep.tile([P, (H + S + EARLY) // 4], I32, name="planes_first", align_bytes=64),
         }
         last_plane = keep.tile([P, S2 // 4], I32, name="last_plane", align_bytes=64)
         w4_raw = keep.tile([P, 2, H // 2], I32, name="w4_raw", align_bytes=64)
@@ -74,7 +76,7 @@ def tile_list_duplicate_collision_score_kernel(
             nc.sync.dma_start(out=dst[:], in_=words.rearrange("p t i -> p (t i)").bitcast(I32))
 
         def load_scale_rows(dst, scales):
-            nc.sync.dma_start(out=dst[0:P:4, :], in_=scales.rearrange("a q n -> (a q) n").bitcast(I32))
+            nc.sync.dma_start(out=dst[32:96:2, :], in_=scales.rearrange("a q n -> q a n").bitcast(I32))
 
         nc.sync.dma_start(out=w4_raw[:], in_=w4_words.rearrange("a p n -> p a n").bitcast(I32))
         nc.sync.dma_start(idx[:], offs)
@@ -104,9 +106,11 @@ def tile_list_duplicate_collision_score_kernel(
             )
             return moved
 
-        def move_scales(plane, picked, a):
+        def move_scales(plane, picked, a, first_row=0):
             for r in range(4):
-                nc.sync.dma_start(out=plane[r:P:32, :], in_=picked[64 * a + 4 * r : 64 * (a + 1) : 16, :].bitcast(I32))
+                nc.sync.dma_start(
+                    out=plane[first_row + r : P : 32, :], in_=picked[32 + 4 * r + 2 * a : 96 : 16, :].bitcast(I32)
+                )
 
         rounded, w1_codes, v_codes, v2_codes = {}, {}, {}, {}
         p_bank, c_bank, tanh_p, h_rounded, h_codes = {}, {}, {}, {}, {}
@@ -194,10 +198,17 @@ def tile_list_duplicate_collision_score_kernel(
         nc.vector.tensor_copy(joined_rows[:, H : H + S].bitcast(I32), v_picked.bitcast(I32))
         move_scales(planes[0], joined_rows[:, : H + S], 0)
         v2_picked = gather(v2_rows[:], idx2, 0, S2, U8, keep.tile([P, S2], U8, name="picked", align_bytes=64)[:])
-        nc.vector.tensor_copy(joined_rows[:, H + S :].bitcast(I32), v2_picked.bitcast(I32))
+        nc.vector.tensor_copy(joined_rows[:, H + S :].bitcast(I32), v2_picked[:, :EARLY].bitcast(I32))
         w4_moved_scales = [planes[g][:].bitcast(U8)[:, :H] for g in range(2)]
         v_scales = [planes[g][:].bitcast(U8)[:, H : H + S] for g in range(2)]
-        v2_scales = {FIRST: planes[FIRST][:].bitcast(U8)[:, H + S :], SECOND: last_plane[:].bitcast(U8)}
+        v2_scales = {}
+        for tile in range(S2 // P):
+            columns = slice(tile * P, (tile + 1) * P)
+            v2_scales[SECOND, tile] = last_plane[:].bitcast(U8)[:, columns]
+            if tile * P < EARLY:
+                v2_scales[FIRST, tile] = planes[FIRST][:].bitcast(U8)[:, H + S :][:, columns]
+            else:
+                v2_scales[FIRST, tile] = last_plane[LATE_ROW:, :].bitcast(U8)[:, columns]
         load_rows(w1_second[FIRST], w1[PASS:, FIRST * PASS : (FIRST + 1) * PASS])
         load_words(v_table[1], tab_words[1])
         move_scales(planes[1], joined_rows, 1)
@@ -205,6 +216,7 @@ def tile_list_duplicate_collision_score_kernel(
         for a in (FIRST, SECOND):
             load_words(v2_table[a], tab2_words[a])
         move_scales(last_plane, v2_picked, SECOND)
+        move_scales(last_plane[:, EARLY // 4 :], v2_picked[:, EARLY:], FIRST, LATE_ROW)
 
         round_w1(0, FIRST, 0, on_vector=False)
         round_w1(0, FIRST, 1, on_vector=False)
@@ -259,12 +271,11 @@ def tile_list_duplicate_collision_score_kernel(
             weighted_code(SECOND, b)
             if b == 0:
                 quantise_h(FIRST, 1)
-            if b == 2:
+            if b == 1:
+                pick_v2_words(FIRST, 0)
                 quantise_h(SECOND, 0)
-        pick_v2_words(FIRST, 0)
+        pick_v2_words(FIRST, 1)
         quantise_h(SECOND, 1)
-        for q in range(1, AHEAD):
-            pick_v2_words(FIRST, q)
 
         score_banks = {(0, half): psum.tile([P, HALF], F32, name="bank%d" % (half * 2 * AHEAD))[:] for half in range(2)}
         for tile in range(1, S2 // P):
@@ -279,7 +290,7 @@ def tile_list_duplicate_collision_score_kernel(
                 nc.tensor.matmul_mx(
                     out=score_banks[tile, half],
                     lhsT=v2_codes[a, q][:, n * P : (n + 1) * P].bitcast(FP8X4),
-                    lhsT_scale=v2_scales[a][:, tile * P : (tile + 1) * P],
+                    lhsT_scale=v2_scales[a, tile],
                     rhs=h_codes[a, half][:].bitcast(FP8X4),
                     rhs_scale=h_scales[:, a, records],
                     start=(a == FIRST and (half == 0 or tile == 0)),

@@ -84,8 +84,10 @@ def tile_list_duplicate_collision_score_kernel(
         load_scale_rows(w4_rows, w4_scales)
         nc.sync.dma_start(idx2[:], offs2)
         nc.sync.dma_start(out=gains[:, :, :4], in_=gain.rearrange("(a p t) -> p a t", a=2, t=4))
+        first_rows = w1[:PASS, :].rearrange("(p j) c -> p j c", j=4)
+        nc.sync.dma_start(out=w1_first[:, :1, :], in_=first_rows[:, :1, :])
         load_scale_rows(v2_rows, tab2_scales)
-        load_rows(w1_first, w1[:PASS, :])
+        nc.sync.dma_start(out=w1_first[:, 1:, :], in_=first_rows[:, 1:, :])
         load_words(v_table[0], tab_words[0])
 
         def vector_tile(width, dtype):

from contextlib import ExitStack

import concourse.mybir as mybir

K, T, S, H, T2, S2 = 1024, 2048, 512, 1024, 4096, 1536
FLOPS = 2 * (2 * K * H * S + H * S2 * S)

F32 = mybir.dt.float32
BF16 = mybir.dt.bfloat16
I32 = mybir.dt.int32
U32 = mybir.dt.uint32
U16 = mybir.dt.uint16
U8 = mybir.dt.uint8
FP8X4 = mybir.dt.float8_e4m3fn_x4
FP4X4 = mybir.dt.float4_e2m1fn_x4
ACT = mybir.ActivationFunctionType
MULT = mybir.AluOpType.mult

P = 128
PASS = 512
PAIR = 2 * P
HALF = S // 2
FIRST, SECOND = 1, 0
AHEAD = 2
EARLY = AHEAD * PAIR
LATE_ROW = 4
VECTOR_TILES = 34
SCALAR_TILES = 15


def tile_list_duplicate_collision_score_kernel(
    tc, tab_words, tab_scales, offs, tab2_words, tab2_scales, offs2, w1, gain, w4_words, w4_scales, out
):
    nc = tc.nc
    with ExitStack() as ctx:
        lists = ctx.enter_context(tc.tile_pool(name="lists", bufs=1))
        keep = ctx.enter_context(tc.tile_pool(name="keep", bufs=1))
        ordered = ctx.enter_context(tc.tile_pool(name="ordered", bufs=1))
        stage = ctx.enter_context(tc.tile_pool(name="stage", bufs=S2 // P))
        psum = ctx.enter_context(tc.psum_pool(name="psum", bufs=1))

        idx = lists.tile([P, S // 16], U16, name="idx")
        idx2 = lists.tile([P, S2 // 16], U16, name="idx2")

        v_rows = keep.tile([P, T // 4], I32, name="v_rows", align_bytes=64)
        w4_rows = keep.tile([P, H // 4], I32, name="w4_rows", align_bytes=64)
        v2_rows = keep.tile([P, T2 // 4], I32, name="v2_rows", align_bytes=64)
        joined_rows = keep.tile([P, H + S + EARLY], U8, name="joined_rows", align_bytes=64)
        planes = {
            SECOND: keep.tile([P, (H + S) // 4], I32, name="planes_second", align_bytes=64),
            FIRST: keep.tile([P, (H + S + EARLY) // 4], I32, name="planes_first", align_bytes=64),
        }
        last_plane = keep.tile([P, S2 // 4], I32, name="last_plane", align_bytes=64)
        w4_raw = keep.tile([P, 2, H // 2], I32, name="w4_raw", align_bytes=64)
        gains = keep.tile([P, 2, 8], F32, name="gains")
        zero_in = keep.tile([P, 1], F32, name="zero_in")
        zero = keep.tile([P, 1], F32, name="zero")
        w1_first = keep.tile([P, 4, H], F32, name="w1_first")
        w1_second = [keep.tile([P, 4, PASS], F32, name="w1_second%d" % a) for a in range(2)]
        w1_rows = {(0, a): w1_first[:, :, a * PASS : (a + 1) * PASS] for a in range(2)}
        w1_rows.update({(1, a): w1_second[a][:] for a in range(2)})
        v_table = [keep.tile([P, T], I32, name="v_table%d" % g, align_bytes=64) for g in range(2)]
        v2_table = [keep.tile([P, T2], I32, name="v2_table%d" % a, align_bytes=64) for a in range(2)]
        w1_scales = keep.tile([P, 2 * H], U8, name="w1_scales", align_bytes=64)
        h_scales = keep.tile([P, 2, S], U8, name="h_scales", align_bytes=64)

        for cleared in (v_rows, w4_rows, v2_rows, planes[0], planes[1], last_plane):
            nc.vector.memset(cleared[:], 0)
        nc.gpsimd.memset(zero_in[:], 0.0)
        nc.scalar.activation(zero[:], zero_in[:], ACT.Tanh)

        def load_rows(dst, rows):
            nc.sync.dma_start(out=dst[:], in_=rows.rearrange("(p j) c -> p j c", j=4))

        def load_words(dst, words):
            nc.sync.dma_start(out=dst[:], in_=words.rearrange("p t i -> p (t i)").bitcast(I32))

        def load_scale_rows(dst, scales):
            nc.sync.dma_start(out=dst[32:96:2, :], in_=scales.rearrange("a q n -> q a n").bitcast(I32))

        nc.sync.dma_start(out=w4_raw[:], in_=w4_words.rearrange("a p n -> p a n").bitcast(I32))
        nc.sync.dma_start(idx[:], offs)
        load_scale_rows(v_rows, tab_scales)
        load_scale_rows(w4_rows, w4_scales)
        nc.sync.dma_start(idx2[:], offs2)
        nc.sync.dma_start(out=gains[:, :, :4], in_=gain.rearrange("(a p t) -> p a t", a=2, t=4))
        first_rows = w1[:PASS, :].rearrange("(p j) c -> p j c", j=4)
        nc.sync.dma_start(out=w1_first[:, :1, :], in_=first_rows[:, :1, :])
        load_scale_rows(v2_rows, tab2_scales)
        nc.sync.dma_start(out=w1_first[:, 1:, :], in_=first_rows[:, 1:, :])
        load_words(v_table[0], tab_words[0])

        def vector_tile(width, dtype):
            return ordered.tile([P, width], dtype, name="vector_out", align_bytes=64, bufs=VECTOR_TILES)

        def scalar_tile(width, dtype):
            return ordered.tile([P, width], dtype, name="scalar_out", align_bytes=64, bufs=SCALAR_TILES)

        def gather(window, offsets, first, count, dtype, picked=None):
            picked = vector_tile(count, dtype)[:] if picked is None else picked
            nc.vector.tensor_copy(picked, window.bitcast(dtype).indirect(offsets[:, first // 16 : (first + count) // 16]))
            return picked

        def reorder_columns(copy, raw, dtype, moved):
            copy(
                out=moved.bitcast(dtype).rearrange("p (b t m) -> p b t m", t=4, m=P),
                in_=raw.bitcast(dtype).rearrange("p (b m t) -> p b t m", t=4, m=P),
            )
            return moved

        def move_scales(plane, picked, a, first_row=0):
            for r in range(4):
                nc.sync.dma_start(
                    out=plane[first_row + r : P : 32, :], in_=picked[32 + 4 * r + 2 * a : 96 : 16, :].bitcast(I32)
                )

        rounded, w1_codes, v_codes, v2_codes = {}, {}, {}, {}
        p_bank, c_bank, tanh_p, h_rounded, h_codes = {}, {}, {}, {}, {}

        def round_w1(g, a, u, on_vector):
            rounded[g, a, u] = (vector_tile if on_vector else scalar_tile)(4 * PAIR, BF16)
            copy = nc.vector.tensor_copy if on_vector else nc.scalar.copy
            copy(
                out=rounded[g, a, u][:].rearrange("p (e m j) -> p m j e", e=2, j=4),
                in_=w1_rows[g, a].rearrange("p j (m t) -> p m j t", t=4)[:, :, :, 2 * u : 2 * u + 2],
            )

        def quantise_w1(g, a, u):
            w1_codes[g, a, u] = vector_tile(PAIR, U32)
            first = g * H + a * PASS + u * PAIR
            nc.vector.quantize_mx(
                out=w1_codes[g, a, u][:].bitcast(FP8X4), scales=w1_scales[:, first : first + PAIR], in_=rounded[g, a, u][:]
            )

        def project(g, a, half):
            for t in range(4):
                if g == 0 and t % 2 == 0:
                    p_bank[a, half, t // 2] = psum.tile([P, 2, HALF], F32, name="bank%d" % (2 * half + t // 2))
                first = g * H + a * PASS + t * P
                nc.tensor.matmul_mx(
                    out=p_bank[a, half, t // 2][:, t % 2, :],
                    lhsT=w1_codes[g, a, t // 2][:, (t % 2) * P : (t % 2 + 1) * P].bitcast(FP8X4),
                    lhsT_scale=w1_scales[:, first : first + P],
                    rhs=v_codes[g, half].bitcast(FP8X4),
                    rhs_scale=v_scales[g][:, half * HALF : (half + 1) * HALF],
                    start=(g == 0 and t % 2 == 0),
                    stop=(g == 1 and t % 2 == 1),
                )

        def signed_weights(g, a, b):
            if g == 0:
                c_bank[a, b] = psum.tile([P, 4, P], F32, name="bank%d" % (4 + b))
            for t in range(4):
                first = a * PASS + t * P
                nc.tensor.matmul_mx(
                    out=c_bank[a, b][:, t, :],
                    lhsT=w4_codes[g][:, 2 * first : 2 * (first + P)].bitcast(FP4X4),
                    lhsT_scale=w4_moved_scales[g][:, first : first + P],
                    rhs=v_codes[g, b // 2][:, (b % 2) * P : (b % 2 + 1) * P].bitcast(FP8X4),
                    rhs_scale=v_scales[g][:, b * P : (b + 1) * P],
                    start=(g == 0 and t == 0),
                    stop=(g == 1 and t == 3),
                )

        def soft_code(a, b):
            tanh_p[a, b] = scalar_tile(4 * P, F32)
            for t in range(4):
                nc.scalar.activation(
                    tanh_p[a, b][:, t * P : (t + 1) * P],
                    p_bank[a, b // 2, t // 2][:, t % 2, (b % 2) * P : (b % 2 + 1) * P],
                    ACT.Tanh,
                    bias=zero[:],
                    scale=gains[:, a, t : t + 1],
                )

        def weighted_code(a, b):
            if b % 2 == 0:
                h_rounded[a, b // 2] = vector_tile(4 * HALF, BF16)
            nc.vector.tensor_tensor(
                out=h_rounded[a, b // 2][:, (b % 2) * 4 * P : (b % 2 + 1) * 4 * P].rearrange("p (n i t) -> p n t i", i=2, t=4),
                in0=c_bank[a, b][:].rearrange("p t (n i) -> p n t i", i=2),
                in1=tanh_p[a, b][:].rearrange("p (t n i) -> p n t i", t=4, i=2),
                op=MULT,
            )

        def quantise_h(a, half):
            h_codes[a, half] = vector_tile(HALF, U32)
            nc.vector.quantize_mx(
                out=h_codes[a, half][:].bitcast(FP8X4),
                scales=h_scales[:, a, half * HALF : (half + 1) * HALF],
                in_=h_rounded[a, half][:],
            )

        def pick_v2_words(a, q):
            v2_codes[a, q] = gather(v2_table[a][:], idx2, q * PAIR, PAIR, U32)

        w4_codes = [reorder_columns(nc.scalar.copy, w4_raw[:, g, :], U16, scalar_tile(2 * H, U8)[:]) for g in range(2)]
        v_picked = gather(v_rows[:], idx, 0, S, U8, keep.tile([P, S], U8, name="picked", align_bytes=64)[:])
        reorder_columns(nc.vector.tensor_copy, w4_rows[:], U8, joined_rows[:, :H])
        nc.vector.tensor_copy(joined_rows[:, H : H + S].bitcast(I32), v_picked.bitcast(I32))
        move_scales(planes[0], joined_rows[:, : H + S], 0)
        v2_picked = gather(v2_rows[:], idx2, 0, S2, U8, keep.tile([P, S2], U8, name="picked", align_bytes=64)[:])
        nc.vector.tensor_copy(joined_rows[:, H + S :].bitcast(I32), v2_picked[:, :EARLY].bitcast(I32))
        w4_moved_scales = [planes[g][:].bitcast(U8)[:, :H] for g in range(2)]
        v_scales = [planes[g][:].bitcast(U8)[:, H : H + S] for g in range(2)]
        v2_scales = {}
        for tile in range(S2 // P):
            columns = slice(tile * P, (tile + 1) * P)
            v2_scales[SECOND, tile] = last_plane[:].bitcast(U8)[:, columns]
            if tile * P < EARLY:
                v2_scales[FIRST, tile] = planes[FIRST][:].bitcast(U8)[:, H + S :][:, columns]
            else:
                v2_scales[FIRST, tile] = last_plane[LATE_ROW:, :].bitcast(U8)[:, columns]
        load_rows(w1_second[FIRST], w1[PASS:, FIRST * PASS : (FIRST + 1) * PASS])
        load_words(v_table[1], tab_words[1])
        move_scales(planes[1], joined_rows, 1)
        load_rows(w1_second[SECOND], w1[PASS:, SECOND * PASS : (SECOND + 1) * PASS])
        for a in (FIRST, SECOND):
            load_words(v2_table[a], tab2_words[a])
        move_scales(last_plane, v2_picked, SECOND)
        move_scales(last_plane[:, EARLY // 4 :], v2_picked[:, EARLY:], FIRST, LATE_ROW)

        round_w1(0, FIRST, 0, on_vector=False)
        round_w1(0, FIRST, 1, on_vector=False)
        round_w1(0, SECOND, 1, on_vector=False)
        quantise_w1(0, FIRST, 0)
        round_w1(0, SECOND, 0, on_vector=True)
        first_pass = gather(v_table[0][:], idx, 0, S, U32)
        v_codes.update({(0, half): first_pass[:, half * HALF : (half + 1) * HALF] for half in range(2)})
        quantise_w1(0, FIRST, 1)
        quantise_w1(0, SECOND, 0)
        for half in range(2):
            project(0, FIRST, half)
        for b in range(4):
            signed_weights(0, FIRST, b)

        round_w1(1, FIRST, 0, on_vector=True)
        round_w1(1, FIRST, 1, on_vector=False)
        quantise_w1(0, SECOND, 1)
        quantise_w1(1, FIRST, 0)
        quantise_w1(1, FIRST, 1)
        for half in range(2):
            v_codes[1, half] = gather(v_table[1][:], idx, half * HALF, HALF, U32)
        for half in range(2):
            project(1, FIRST, half)
            signed_weights(1, FIRST, 2 * half)
            signed_weights(1, FIRST, 2 * half + 1)

        for b in range(2):
            soft_code(FIRST, b)
            weighted_code(FIRST, b)
        round_w1(1, SECOND, 1, on_vector=False)
        round_w1(1, SECOND, 0, on_vector=True)
        quantise_h(FIRST, 0)
        for u in range(2):
            quantise_w1(1, SECOND, u)
        for b in range(2, 4):
            soft_code(FIRST, b)
            weighted_code(FIRST, b)

        project(0, SECOND, 0)
        for b in range(2):
            for g in range(2):
                signed_weights(g, SECOND, b)
        project(1, SECOND, 0)
        for g in range(2):
            project(g, SECOND, 1)
        for b in range(2, 4):
            for g in range(2):
                signed_weights(g, SECOND, b)
        for b in range(4):
            soft_code(SECOND, b)
            weighted_code(SECOND, b)
            if b == 0:
                quantise_h(FIRST, 1)
            if b == 1:
                pick_v2_words(FIRST, 0)
                quantise_h(SECOND, 0)
        pick_v2_words(FIRST, 1)
        quantise_h(SECOND, 1)

        score_banks = {(0, half): psum.tile([P, HALF], F32, name="bank%d" % (half * 2 * AHEAD))[:] for half in range(2)}
        for tile in range(1, S2 // P):
            bank = psum.tile([P, S], F32, name="bank%d" % (tile % (2 * AHEAD)))
            score_banks.update({(tile, half): bank[:, half * HALF : (half + 1) * HALF] for half in range(2)})
            score_banks[tile, "whole"] = bank[:]

        def score_pass(tile, a):
            q, n = divmod(tile, 2)
            for half in range(2):
                records = slice(half * HALF, (half + 1) * HALF)
                nc.tensor.matmul_mx(
                    out=score_banks[tile, half],
                    lhsT=v2_codes[a, q][:, n * P : (n + 1) * P].bitcast(FP8X4),
                    lhsT_scale=v2_scales[a, tile],
                    rhs=h_codes[a, half][:].bitcast(FP8X4),
                    rhs_scale=h_scales[:, a, records],
                    start=(a == FIRST and (half == 0 or tile == 0)),
                    stop=(a == SECOND and (half == 1 or tile == 0)),
                )

        def store_scores(tile):
            score = stage.tile([P, S], F32, name="score")
            rows = slice(tile * P, (tile + 1) * P)
            parts = {0: slice(0, HALF), 1: slice(HALF, S)} if tile == 0 else {"whole": slice(0, S)}
            for part, records in parts.items():
                nc.scalar.activation(score[:, records], score_banks[tile, part], ACT.Abs)
                nc.sync.dma_start(out=out[rows, records], in_=score[:, records])

        for tile in range(2 * AHEAD):
            score_pass(tile, FIRST)
        for q in range(S2 // PAIR):
            if q >= AHEAD:
                pick_v2_words(FIRST, q)
            pick_v2_words(SECOND, q)
            for tile in (2 * q, 2 * q + 1):
                if q >= AHEAD:
                    score_pass(tile, FIRST)
                score_pass(tile, SECOND)
                store_scores(tile)
